import numpy as np, ml_dtypes
CORES = [2,3,42,43,82,83,122,123]
N = 8
import mx_ref
BF = ml_dtypes.bfloat16
def f(rng, *shape):
    return mx_ref.flush((rng.standard_normal(shape, dtype=np.float32) * np.exp2(rng.integers(-2, 3, shape[:-1] + (1,)))).astype(BF))
def wide(rng, *shape, cols=0):
    v = rng.standard_normal(shape, dtype=np.float32) * np.exp2(rng.integers(-12, 13, shape)).astype(np.float32)
    if cols: v *= np.repeat(np.exp2(rng.integers(-cols, cols + 1, shape[:-2] + (1, shape[-1] // 4))) * (rng.random(shape[:-2] + (1, shape[-1] // 4)) > 0.0625), 4, axis=-1).astype(np.float32)
    return mx_ref.flush(v.astype(BF))
T, CAPP, O = 512, 96, 1
def scores(us, x):
    return mx_ref.matmul(mx_ref.quantize(us), mx_ref.quantize(x))[:8] + np.float32(0.0)
def winners(us, x):
    return np.argmax(np.stack([scores(us[s], x[s]) for s in range(N)]), axis=0)
def fill(rng, n, tot, most):
    n = np.array(n)
    while n.sum() < tot:
        q = rng.integers(0, N)
        if n[q] < most[q]: n[q] += 1
    return rng.permutation(np.repeat(np.arange(N), n))
def deal(rng, full):
    return np.stack([fill(rng, [CAPP if q in full[g] else 0 for q in range(N)], T, [CAPP] * N) for g in range(8)])
def one(rng):
    g, s = rng.integers(0, 8), rng.integers(0, N)
    return deal(rng, [[s] if i == g else [] for i in range(8)])
def heads(rng):
    u, h = np.zeros((8, 16, 128, 4), np.float32), np.arange(8)
    u[h, :, h] = rng.choice([-1.0, 1.0], (8, 16, 4)) * (0.25 + np.abs(rng.standard_normal((8, 16, 4)))) * np.exp2(rng.integers(-2, 3, (8, 16, 1)))
    return np.repeat(u.reshape(1, 128, 512).astype(BF), N, axis=0)
def plant(rng, x, us, wn, big=4, tie=None, zero=None):
    v = np.abs(x.astype(np.float32)).reshape(N, 8, 16, T, 4)
    v[v < 2.0 ** -24] = 0
    h, b = np.arange(8), np.float32(big)
    a = np.sign(us.astype(np.float32)).reshape(8, 16, 128, 4)[h, :, h][:, :, None]
    win = (wn == np.arange(N)[:, None, None])[:, :, None, :, None]
    neg = (rng.random((8, T)) < 0.125)[:, None, :, None]
    c = np.where(rng.random(v.shape, dtype=np.float32) < 0.5, np.float32(-1), np.float32(1))
    t = (np.where(neg, np.where(win, -a, -4 * b * a), np.where(win, b * a, c)) * v).astype(np.float32)
    s = np.stack([scores(us, t[r].reshape(128, 4 * T).astype(BF)) for r in range(N)])
    won = np.take_along_axis(s, wn[None], axis=0)[0]
    lost = np.where(win[:, :, 0, :, 0], -np.inf, s).max(axis=0)
    bad = (~(won - lost > 0.5 * np.abs(won)))[:, None, :, None]
    t = np.where(bad, np.where(win, b * a, -a) * v, t).astype(np.float32)
    if tie is not None:
        best = np.where(win, t, np.float32(0)).sum(axis=0)
        t = np.where(tie[:, None, :, None] & (wn < np.arange(N)[:, None, None])[:, :, None, :, None], best, t)
    if zero is not None: t[:, :, :, zero] = 0
    return t.reshape(N, 128, 4 * T).astype(BF)
def narrow(rng, x, us, wn):
    v, h = x.astype(np.float32).reshape(N, 8, 16, T, 4), np.arange(8)
    u = np.abs(us.astype(np.float32)).reshape(8, 16, 128, 4)[h, :, h]
    i, b = np.unravel_index(u.reshape(8, 64).argmin(axis=1), (16, 4))
    win = wn == np.arange(N)[:, None, None]
    part = np.where(win[:, :, None, :, None], v, np.float32(0)).sum(axis=0)
    p = np.exp2(np.floor(np.log2((u[:, :, None] * np.abs(part)).sum(axis=(1, 3))) - np.log2(u[h, i, b])[:, None]) - 12)
    z = np.stack([np.where(part[g, i[g], :, b[g]] < 0, -p[g], p[g]) for g in range(8)])
    close = np.repeat((rng.permutation(T) < T // 3)[None], 8, axis=0)
    other = (wn + rng.integers(1, N, (8, T))) % N
    hold = ((rng.random((N, 8, T)) < 0.25) | (other == np.arange(N)[:, None, None])) & ~win & close
    held = hold | (win & close)
    t = np.where(held[:, :, None, :, None], part, v).astype(np.float32)
    d = np.where(hold, rng.choice([-0.125, 0.125], (N, 8, T)), 0.0)
    for k in range(2):
        for g in range(8): t[:, g, i[g], :, b[g]] = np.where(held[:, g], z[g] * (1.5 + d[:, g]), t[:, g, i[g], :, b[g]])
        s = np.stack([scores(us, t[r].reshape(128, 4 * T).astype(BF)) for r in range(N)])
        if k == 0: d = np.where(s == np.take_along_axis(s, wn[None], axis=0), 2 * d, d)
    now = np.argmax(s, axis=0)
    for g in range(8):
        for k in range(T):
            n = np.bincount(now[g], minlength=N)
            q = n.argmax()
            if n[q] <= CAPP: break
            j = rng.permutation(np.flatnonzero((now[g] == q) & (wn[g] != q)))[:n[q] - CAPP]
            now[g, j] = wn[g, j]; close[g, j] = False
    return np.where(close[:, None, :, None], t, v).reshape(N, 128, 4 * T).astype(BF)
def draw(rng, wn, **k):
    us = heads(rng)
    return {"x": plant(rng, f(rng, N, 128, 4 * T), us[0], wn, **k), "us": us, "w": f(rng, N, 128, 512 * O)}
def setup_inputs(rng):
    return draw(rng, one(rng))
def setup_inputs_equal(rng):
    e, p = CAPP - 8, rng.permutation(T)
    far = np.stack([fill(rng, [8] + [0] * (N - 1), T - e, [8] + [CAPP] * (N - 1)) for g in range(8)])
    wn = np.concatenate([np.zeros((8, e), int), far], axis=1)[:, p]
    tie = np.repeat(np.concatenate([np.ones(e, bool), np.arange(T - e) % 2 == 0])[None], 8, axis=0)[:, p]
    return draw(rng, wn, tie=tie, zero=(np.arange(T) < 4)[p])
def setup_inputs_full(rng):
    s, k = int(rng.integers(0, N)), T // CAPP
    return draw(rng, deal(rng, [[s] + [q for q in rng.permutation(N).tolist() if q != s][:k - 1] for g in range(8)]))
def setup_inputs_near(rng):
    wn = one(rng)
    d = draw(rng, wn); d["x"] = narrow(rng, d["x"], d["us"][0], wn); return d
def setup_inputs_spread(rng):
    wn, us = one(rng), heads(rng)
    e = np.exp2(rng.integers(-4, 5, (N, 8, 1, T, 1))) * ((rng.random((N, 8, 1, T, 1)) > 0.0625) | (wn == np.arange(N)[:, None, None])[:, :, None, :, None])
    x = wide(rng, N, 128, 4 * T).astype(np.float32).reshape(N, 8, 16, T, 4) * e.astype(np.float32)
    return {"x": plant(rng, x, us[0], wn, big=256), "us": us, "w": f(rng, N, 128, 512 * O)}
def setup_inputs_stretch(rng):
    L = []
    for g in range(8):
        s, a = rng.integers(0, N), rng.choice([0, T - CAPP, rng.integers(0, T - CAPP + 1)])
        far = fill(rng, [0] * N, T - CAPP, [0 if q == s else CAPP for q in range(N)])
        L.append(np.concatenate([far[:a], np.full(CAPP, s), far[a:]]))
    return draw(rng, np.stack(L))
def check_inputs(d):
    b = []
    for k in ("x", "us", "w"):
        v = np.abs(np.asarray(d[k]).astype(np.float32))
        if not ((v == 0) | ((v >= 2.0 ** -30) & (v <= 2.0 ** 30))).all(): b.append(k)
    if b: return b
    u, h = np.array(d["us"]).astype(np.float32), np.arange(8)
    same = (u == u[:1]).all()
    u = u.reshape(N, 8, 16, 128, 4); u[:, h, :, h] = 0
    if not same or (u != 0).any(): b.append("us")
    wn = winners(d["us"], d["x"])
    if max((wn == s).sum(axis=1).max() for s in range(N)) > CAPP: b.append("x")
    return b
def reference(x, us, w):
    wn = winners(us, x)
    M = []
    for s in range(N):
        v = np.where((wn == s)[:, None, :, None], x[s].astype(np.float32).reshape(8, 16, T, 4), np.float32(0))
        M.append(mx_ref.quantize(np.ascontiguousarray(v.reshape(128, 4 * T).astype(BF))))
    y = np.zeros((N, 128, O * T), np.float32)
    for r in range(N):
        for o in range(O):
            W = mx_ref.quantize(np.ascontiguousarray(w[r][:, 512 * o:512 * o + 512]))
            for s in range(N): y[r][:, T * o:T * o + T] += mx_ref.matmul(W, M[s])
    return {"y": y, "wn": np.repeat(wn.astype(np.float32)[None], N, axis=0)}

@@ -1,0 +1,315 @@
+from concourse.bass import DstId, RemoteDMATransfer
+from concourse.mybir import dt, AluOpType, ActivationFunctionType
+
+F4, F, B = "float8_e4m3fn_x4", "float32", "bfloat16"
+SCRATCH = {}
+for _names, _w, _t in (
+        ("uw", 64, B), ("xs", 2048, B), ("zt", 560, B), ("wz", 4096, B), ("h", 512, B),
+        ("cz", 140, F4), ("pz", 140, "uint8"), ("cx", 512, F4), ("px", 512, "uint8"), ("cw", 1024, F4), ("pw", 1024, "uint8"),
+        ("ca", 224, F4), ("pa", 224, "uint8"), ("cb", 576, F4), ("pb", 576, "uint8"),
+        ("ia ib", 4, "int32"), ("fa", 4, F), ("g8 kc st1 st2", 8, F), ("v32 ms sm m1 b1 g2 x1 y1", 128, F),
+        ("oz", 36, "uint16"), ("ic c1 i16 r16 one", 32, F), ("ij cj ya", 512, F), ("k4 m4 r4 lm ls", 96, F),
+        ("i256 wt r ep u uv wv bx", 256, F), ("r256 ee cs8", 256, B), ("s2 m2 e3b b2 x2 y2", 64, F), ("l", 528, F),
+        ("e1 e2 e3 e12 e cs t1 t2 t3 v1 v3 tt tu tv tw ix it win", 32, F),
+        ("ow", 32, "uint16"), ("og", 24, "uint16"), ("off", 256, "uint16"), ("p", 6144, F)):
+    for _k in _names.split():
+        SCRATCH[_k] = ("sbuf", [128, _w], _t)
+SCRATCH["ps"] = ("psum", [128, 4096], F)
+SEMAPHORES = ["lu", "lx0", "lx1", "lx2", "lx3", "lw", "gi", "v", "s", "pe", "it1", "it2", "st",
+              "asc", "aa", "aap", "ab", "abp", "ac", "loc"]
+
+ADD, SUB, MUL, MAX, MIN = AluOpType.add, AluOpType.subtract, AluOpType.mult, AluOpType.max, AluOpType.min
+GE, GT, EQ, AND = AluOpType.is_ge, AluOpType.is_gt, AluOpType.is_equal, AluOpType.bitwise_and
+COPY = ActivationFunctionType.Copy
+
+
+def bitrev(s):
+    return (s & 1) * 4 + (s & 2) + (s >> 2)
+
+
+def rank_program(g, core, T, topo):
+    rank = T.rank_of(core)
+    if rank is None:
+        return
+    S = T.sem
+    V, A, P, Y = g.vector, g.scalar, g.tensor, g.sync
+    n = {"v": 0, "s": 0, "pe": 0, "gi": 0, "loc": 0}
+
+    def inc(q, call):
+        n[q] += 1
+        call.then_inc(S[q], 1)
+        return n[q]
+
+    vw = lambda k: V.wait_ge(S.v, k)
+    vec = lambda call: inc("v", call)
+    tt = lambda out, a, b, op: vec(V.tensor_tensor(out, a, b, op))
+    ts = lambda out, a, s1, op, s2=None, op2=None: vec(V.tensor_scalar(out, a, s1, s2, op, op2) if op2 else V.tensor_scalar(out, a, s1, None, op))
+    scan = lambda out, a, b, o0=MUL, o1=ADD: vec(V.tensor_tensor_scan(out, a, b, 0.0, o0, o1))
+    iota = lambda out, pat, base, cm: inc("gi", g.iota(out, pat, base, cm, allow_small_or_imprecise_dtypes=True))
+
+    cores = list(T.cores)
+    chips = []
+    for c in cores:
+        if topo.chip(c) not in chips:
+            chips.append(topo.chip(c))
+    on = lambda ch: [c for c in cores if topo.chip(c) == ch]
+    mychip = topo.chip(core)
+    kind = on(mychip).index(core)
+    mate = [c for c in on(mychip) if c != core][0]
+    far = [c for c in cores if topo.chip(c) != mychip]
+    same = [on(ch)[kind] for ch in chips if ch != mychip]
+    slot = lambda frm, to: 192 * [ch for ch in chips if ch != topo.chip(to)].index(topo.chip(frm))
+    eng_far = [e for e in topo.engines(core, mate) if all(e in topo.engines(core, c) for c in far)]
+    eng_near = [e for e in topo.engines(core, mate) if e not in eng_far][:4]
+    n_far, n_near = len(eng_far), len(eng_near)
+    did = lambda c: DstId(rid=topo.addr(c)[0], pnc=topo.addr(c)[1])
+
+    def start_of(s):
+        c = cores[s]
+        if c in (core, mate):
+            return 0 if c == core else 96
+        return 192 + slot(c, core) + (0 if c in same else 96)
+
+    def send(*transfers):
+        n["loc"] += sum(len(m) for m, _, _, _ in transfers)
+        g.remote_dma_fused([RemoteDMATransfer(dst_ids=[did(c) for c, _ in to], dma_engine_mask=sum(1 << e for e in m), remote_sem=sem,
+                                              srcs=[src], dsts=[d for _, d in to], alu_op=0) for m, sem, src, to in transfers], local_sem=S.loc)
+
+    Y.dma_start(T.uw[:, 0:64], T.us[:, 0:64]).then_inc(S.lu, 16)
+    for q, k in ((A, 0), (Y, 1), (A, 2), (Y, 3)):
+        q.dma_start(T.xs[:, 512 * k:512 * k + 512], T.x[:, 512 * k:512 * k + 512]).then_inc(S["lx%d" % k], 16)
+
+    inc("gi", g.iota(T.ia[:, 0:1], [[0, 1]], 0, 1))
+    inc("gi", g.iota(T.ia[:, 1:2], [[0, 1]], 0, 32))
+    k_a = iota(T.g8[:, :], [[4, 8]], 0, 0)
+    k_b = iota(T.v32[:, :], [[1, 4], [0, 32]], 0, 0)
+    iota(T.ic[:, :], [[-1, 32]], 512, 0)
+    iota(T.k4[:, :], [[0, 24], [1, 4]], 0, 0)
+    iota(T.i16[:, :], [[0, 2], [1, 16]], 0, 0)
+    iota(T.ij[:, :], [[4, 32], [128, 16]], 0, 0)
+    k_c = iota(T.i256[:, :], [[0, 8], [1, 32]], 0, 0)
+
+    vec(V.memset(T.oz[:, :], 32))
+    v_z = vec(V.memset(T.wz[:, 0:1024], 0.0))
+    A.wait_ge(S.v, v_z)
+    s_wz = inc("s", A.activation(T.wz[:, 3072:4096], T.wz[:, 0:1024], COPY))
+    V.wait_ge(S.gi, k_a)
+    ts(T.ib[:, 0:1], T.ia[:, 0:1], 3, AND)
+    ts(T.ib[:, 1:2], T.ia[:, 1:2], 511, AND)
+    vw(ts(T.ib[:, 2:3], T.ia[:, 0:1], 12, AND, 2, AluOpType.arith_shift_right))
+    vw(vec(V.tensor_copy(T.fa[:, 0:3], T.ib[:, 0:3])))
+    v_oz = ts(T.oz[:, 3:32:4], T.g8[:, :], T.fa[:, 0:1], ADD)
+    vec(V.memset(T.wz[:, 1024:2048], 0.0))
+    V.wait_ge(S.gi, k_b)
+    ts(T.ms[:, :], T.v32[:, :], T.fa[:, 0:1], EQ)
+
+    A.wait_ge(S.lu, 16)
+    A.wait_ge(S.v, v_oz)
+    s_zt = inc("s", A.activation(T.zt[:, :], T.uw[:, 0:64].indirect(T.oz[:, 0:35]), COPY))
+
+    for q in range(4):
+        if q == 3:
+            V.wait_ge(S.s, s_zt)
+            vec(V.quantize_mx(T.cz[:, :], T.pz[:, :], T.zt[:, :]))
+        V.wait_ge(S["lx%d" % q], 16)
+        v_x = vec(V.quantize_mx(T.cx[:, 128 * q:128 * q + 128], T.px[:, 128 * q:128 * q + 128], T.xs[:, 512 * q:512 * q + 512]))
+        if q == 0:
+            v_wz = vec(V.memset(T.wz[:, 2048:3072], 0.0))
+    for q in range(4):
+        a, b = 12 - 4 * q, 128 * q
+        P.wait_ge(S.v, v_x if q == 3 else v_x - 1)
+        k_sc = inc("pe", P.matmul_mx(T.ps[:, 3584:3712], T.cz[:, a:a + 128], T.pz[:, a:a + 128],
+                                     T.cx[:, b:b + 128], T.px[:, b:b + 128], q == 0, q == 3))
+
+    Y.wait_ge(S.v, v_wz)
+    Y.wait_ge(S.s, s_wz)
+    for q in range(8):
+        Y.dma_start(T.wz[16 * q:16 * q + 16, 512 * q:512 * q + 512], T.w[16 * q:16 * q + 16, :]).then_inc(S.lw, 16)
+
+    V.wait_ge(S.pe, k_sc)
+    me = bitrev(rank)
+    R = lambda b, q=1: T.r[:, 32 * b:32 * (b + q)]
+    own = R(me)
+    vw(tt(T.sm[:, :], T.ps[:, 3584:3712], T.ms[:, :], MUL))
+    vw(tt(T.s2[:, :], T.sm[:, 0:64], T.sm[:, 64:128], ADD))
+    g.wait_ge(S.v, tt(own, T.s2[:, 0:32], T.s2[:, 32:64], ADD))
+    near2 = eng_near[:2]
+    send((eng_far, S.asc, own, [(c, own) for c in far]), (near2, S.asc, own, [(mate, own)]))
+
+    vec(V.memset(T.h[:, 0:128], 0.0))
+    V.wait_ge(S.gi, k_c)
+    ts(T.c1[:, :], T.ic[:, :], T.fa[:, 1:2], SUB)
+    ts(T.cj[:, :], T.ij[:, :], T.fa[:, 0:1], ADD)
+    ts(T.m4[:, :], T.k4[:, :], T.fa[:, 2:3], EQ)
+    ts(T.r4[:, :], T.k4[:, :], 1.0, MIN)
+    ts(T.r16[:, :], T.i16[:, :], 1.0, MIN)
+    ts(T.r256[:, :], T.i256[:, :], 1.0, MIN)
+    vec(V.memset(T.one[:, :], 1.0))
+    vec(V.memset(T.tt[:, :], 0.0))
+    for b in range(8):
+        vec(V.memset(T.kc[:, b:b + 1], float(start_of(bitrev(b)) + 96)))
+        vec(V.memset(T.wt[:, 32 * b:32 * b + 32], float(bitrev(b))))
+    V.wait_ge(S.lw, 128)
+    vec(V.quantize_mx(T.cw[:, 0:512], T.pw[:, 0:512], T.wz[:, 0:2048]))
+    vec(V.quantize_mx(T.cw[:, 512:1024], T.pw[:, 512:1024], T.wz[:, 2048:4096]))
+
+    V.wait_ge(S.asc, n_far * len(far) + len(near2))
+    vw(n["v"])
+    half = lambda t, k: t[:, 32 * k:32 * k + 32]
+    two = lambda t, k: t[:, 64 * k:64 * k + 64]
+    lo, hi = me & 3, me & 1
+    v_m1 = tt(T.m1[:, :], R(0, 4), R(4, 4), MAX)
+    tt(T.e1[:, :], own, R(me ^ 4), GT if me & 4 else GE)
+    vw(v_m1)
+    v_m2 = tt(T.m2[:, :], T.m1[:, 0:64], T.m1[:, 64:128], MAX)
+    v_e2 = tt(T.e2[:, :], half(T.m1, lo), half(T.m1, lo ^ 2), GT if me & 2 else GE)
+    vw(v_m2)
+    tt(T.e3[:, :], half(T.m2, hi), half(T.m2, hi ^ 1), GT if me & 1 else GE)
+    vw(v_e2)
+    v_e12 = tt(T.e12[:, :], T.e1[:, :], T.e2[:, :], MUL)
+    tt(half(T.e3b, 0), half(T.m2, 0), half(T.m2, 1), GE)
+    vw(v_e12)
+    v_e = tt(T.e[:, :], T.e12[:, :], T.e3[:, :], MUL)
+    tt(half(T.e3b, 1), half(T.m2, 1), half(T.m2, 0), GT)
+    vw(v_e)
+    v_cs = scan(T.cs[:, :], T.one[:, :], T.e[:, :], ADD, SUB)
+    v_v1 = tt(T.v1[:, :], T.e[:, :], T.c1[:, :], MUL)
+    vw(v_cs)
+    v_t1 = vec(V.transpose(T.t1[:, :], T.cs[:, :]))
+    vw(v_v1)
+    tt(T.v3[:, :], T.v1[:, :], T.cs[:, :], ADD)
+    vw(v_t1)
+    v_t2 = scan(T.t2[:, :], T.r16[:, :], T.t1[:, :])
+    v_b2 = tt(T.b2[:, :], T.m1[:, 64:128], T.m1[:, 0:64], GT)
+    vw(v_t2)
+    v_t3 = vec(V.transpose(T.t3[:, :], T.t2[:, :]))
+    vw(v_b2)
+    v_g2 = tt(T.g2[:, 64:128], T.e3b[:, :], T.b2[:, :], MUL)
+    vw(v_t3)
+    v_ow = ts(T.ow[:, :], T.v3[:, :], T.t3[:, 31:32], ADD, T.cs[:, 31:32], SUB)
+    vw(v_g2)
+    tt(T.g2[:, 0:64], T.e3b[:, :], T.g2[:, 64:128], SUB)
+    vw(v_ow)
+    v_l = vec(V.tensor_copy(T.l[:, 0:528].indirect(T.ow[:, 0:32]), T.cj[:, :]))
+    v_b1 = tt(T.b1[:, :], R(4, 4), R(0, 4), GT)
+    vw(v_l)
+    v_lm = tt(T.lm[:, :], T.l[:, 417:513], T.m4[:, :], MUL)
+    vw(v_b1)
+    v_eh = tt(T.ee[:, 128:256], T.g2[:, :], T.b1[:, :], MUL)
+    vw(v_lm)
+    v_ls = scan(T.ls[:, :], T.r4[:, :], T.lm[:, :])
+    vw(v_eh)
+    v_ee = tt(T.ee[:, 0:128], T.g2[:, :], T.ee[:, 128:256], SUB)
+    A.wait_ge(S.v, v_ee)
+    s_ep = inc("s", A.activation(T.ep[:, :], T.ee[:, :], COPY))
+    vw(v_ls)
+    v_og = vec(V.tensor_copy(T.og[:, :], T.ls[:, 3:96:4]))
+    A.wait_ge(S.v, v_og)
+    s_h = inc("s", A.activation(T.h[:, 320:512], T.xs[:, 0:2048].indirect(T.og[:, 12:24]), COPY))
+    vw(v_ee)
+    v_cs8 = scan(T.cs8[:, :], T.r256[:, :], T.ee[:, :], MUL, SUB)
+    vw(v_og)
+    v_h = vec(V.tensor_copy(T.h[:, 128:320], T.xs[:, 0:2048].indirect(T.og[:, 0:12])))
+    vw(v_cs8)
+    v_tt = vec(V.tensor_copy(T.tt[:, 0:8], T.cs8[:, 31:256:32]))
+    vw(v_h)
+    V.wait_ge(S.s, s_h)
+    v_q = vec(V.quantize_mx(T.ca[:, 0:128], T.pa[:, 0:128], T.h[:, :]))
+    g.wait_ge(S.v, v_q)
+    by = lambda t, a: t[:, a:a + 96].bitcast(dt.uint8)
+    send((eng_far, S.ab, by(T.ca, 32), [(c, by(T.cb, slot(core, c))) for c in same]),
+         (eng_near, S.aa, by(T.ca, 32), [(mate, by(T.ca, 128))]))
+    send((eng_near, S.aap, T.pa[:, 32:128], [(mate, T.pa[:, 128:224])]))
+    g.wait_ge(S.aap, n_near)
+    send((eng_far, S.abp, T.pa[:, 32:224], [(c, T.pb[:, slot(core, c):slot(core, c) + 192]) for c in same]))
+    g.wait_ge(S.ab, n_far * len(same))
+    on_with = [eng_far[:n_far // 2], eng_far[n_far // 2:], eng_near]
+    send(*[(on_with[k], S.ac, by(T.cb, 192 * k), [(mate, by(T.cb, 192 * k + 96))]) for k in range(len(same))])
+
+    freed = [None] * 8
+
+    def product(q, bank, codes, plane, a, w, skip, at):
+        if freed[bank]:
+            P.wait_ge(S.s, freed[bank])
+        c = 512 * bank
+        k = inc("pe", P.matmul_mx(T.ps[:, c:c + w], T.cw[:, 128 * q:128 * q + 128], T.pw[:, 128 * q:128 * q + 128],
+                                  codes[:, a:a + w], plane[:, a:a + w], True, True))
+        A.wait_ge(S.pe, k)
+        freed[bank] = inc("s", A.activation(T.p[:, 768 * q + at:768 * q + at + w - skip], T.ps[:, c + skip:c + w], COPY))
+        return freed[bank]
+
+    P.wait_ge(S.v, v_q)
+    for q in range(8):
+        product(q, q, T.ca, T.pa, 0, 128, 32, 0)
+
+    vw(v_tt)
+    v_tu = vec(V.transpose(T.tu[:, :], T.tt[:, :]))
+    tt(T.st1[:, :], T.kc[:, :], T.tt[:, 0:8], SUB)
+    vw(v_tu)
+    vw(scan(T.tv[:, :], T.r16[:, :], T.tu[:, :]))
+    vw(vec(V.transpose(T.tw[:, :], T.tv[:, :])))
+    vw(tt(T.st2[:, :], T.st1[:, :], T.tw[:, 0:8], ADD))
+    V.wait_ge(S.s, s_ep)
+    vw(tt(T.ep[:, 0:256:32], T.ep[:, 0:256:32], T.st2[:, :], SUB))
+    vw(scan(T.u[:, :], T.r256[:, :], T.ep[:, :], MUL, SUB))
+    vw(tt(T.uv[:, :], T.u[:, :], T.ee[:, :], MUL))
+    vw(tt(T.x1[:, :], T.uv[:, 0:128], T.uv[:, 128:256], ADD))
+    vw(tt(T.x2[:, :], T.x1[:, 0:64], T.x1[:, 64:128], ADD))
+    vw(tt(T.ix[:, :], T.x2[:, 0:32], T.x2[:, 32:64], ADD))
+    v_it = vec(V.transpose(T.it[:, :], T.ix[:, :]))
+    for q, b in ((Y, 0), (A, 1)):
+        q.wait_ge(S.v, v_it)
+        for k in range(4):
+            q.dma_start(T.bx[0:16, 128 * b + 32 * k:128 * b + 32 * k + 32], T.it[32 * k + 16 * b:32 * k + 16 * b + 16, :]).then_inc(S.it1, 16)
+    Y.wait_ge(S.it1, 128)
+    for q in range(1, 8):
+        Y.dma_start(T.bx[16 * q:16 * q + 16, :], T.bx[0:16, :]).then_inc(S.it2, 16)
+    vw(tt(T.wv[:, :], T.ee[:, :], T.wt[:, :], MUL))
+    vw(tt(T.y1[:, :], T.wv[:, 0:128], T.wv[:, 128:256], ADD))
+    vw(tt(T.y2[:, :], T.y1[:, 0:64], T.y1[:, 64:128], ADD))
+    Y.wait_ge(S.v, tt(T.win[:, :], T.y2[:, 0:32], T.y2[:, 32:64], ADD))
+    Y.dma_start(T.wn[:, :], T.win[:, :]).then_inc(S.st, 16)
+
+    P.wait_ge(S.aap, n_near)
+    P.wait_ge(S.aa, n_near)
+    for q in range(8):
+        product(q, q, T.ca, T.pa, 96, 128, 32, 96)
+    V.wait_ge(S.it1, 128)
+    V.wait_ge(S.it2, 112)
+    vec(V.tensor_copy(T.off[:, 0:256:2], T.bx[:, 0:128]))
+    v_off = vec(V.tensor_copy(T.off[:, 1:256:2], T.bx[:, 128:256]))
+    pick_of = lambda q, a, b: T.p[:, 768 * q:768 * q + 768].indirect(T.off[:, 32 * q + a // 16:32 * q + b // 16])
+    P.wait_ge(S.ab, n_far * len(same))
+    P.wait_ge(S.abp, n_far * len(same))
+    P.wait_ge(S.ac, n_far + n_near)
+    ready = []
+    for q in range(8):
+        ready.append([product(q, (2 * q + k) % 8, T.cb, T.pb, 288 * k, 288, 0, 192 + 288 * k) for k in range(2)][1])
+        if q == 1:
+            A.wait_ge(S.v, v_off)
+            A.wait_ge(S.s, ready[0])
+            s_half = inc("s", A.activation(T.ya[:, 256:512], pick_of(0, 256, 512), COPY))
+
+    vw(v_off)
+
+    def pick(q, a, b, last):
+        out = T.ya[:, a:b]
+        V.wait_ge(S.s, ready[q])
+        if last:
+            vw(last)
+        return vec(V.tensor_tensor(out, pick_of(q, a, b), out, ADD) if last else V.tensor_copy(out, pick_of(q, a, b)))
+
+    last = pick(1, 0, 256, pick(0, 0, 256, 0))
+    V.wait_ge(S.s, s_half)
+    last = pick(1, 256, 512, last)
+    for q in range(2, 6):
+        last = pick(q, 0, 512, last)
+    for a in (0, 256):
+        k = pick(7, a, a + 256, pick(6, a, a + 256, last))
+        Y.wait_ge(S.v, k)
+        Y.dma_start(T.y[:, a:a + 256], T.ya[:, a:a + 256]).then_inc(S.st, 16)
+    Y.wait_ge(S.st, 48)
+    g.wait_ge(S.loc, n["loc"])
+    g.wait_ge(S.v, n["v"])
+    g.wait_ge(S.s, n["s"])
+    g.wait_ge(S.pe, n["pe"])

@@ -5,21 +5,21 @@ F4, F, B = "float8_e4m3fn_x4", "float32", "bfloat16"
 SCRATCH = {}
 for _names, _w, _t in (
         ("uw", 64, B), ("xs", 2048, B), ("zt", 560, B), ("wz", 4096, B), ("h", 512, B),
-        ("cz", 140, F4), ("pz", 140, "uint8"), ("cx", 512, F4), ("px", 512, "uint8"), ("cw", 1024, F4), ("pw", 1024, "uint8"),
-        ("ca", 224, F4), ("pa", 224, "uint8"), ("cb", 576, F4), ("pb", 576, "uint8"),
+        ("cz", 140, F4), ("pz", 140, "uint8"), ("cx", 512, F4), ("cw", 1024, F4), ("pw", 1024, "uint8"),
+        ("ca", 256, F4), ("pa", 1216, "uint8"), ("cb", 576, F4), ("pb", 576, "uint8"),
         ("ia ib", 4, "int32"), ("fa", 4, F), ("g8 kc st1 st2", 8, F), ("v32 ms sm m1 b1 g2 x1 y1", 128, F),
-        ("oz", 36, "uint16"), ("ic c1 i16 r16 one", 32, F), ("ij cj ya", 512, F), ("k4 m4 r4 lm ls", 96, F),
-        ("i256 wt r ep u uv wv bx", 256, F), ("r256 ee cs8", 256, B), ("s2 m2 e3b b2 x2 y2", 64, F), ("l", 528, F),
-        ("e1 e2 e3 e12 e cs t1 t2 t3 v1 v3 tt tu tv tw ix it win", 32, F),
+        ("oz", 36, "uint16"), ("ic c1 i16 r16 one", 32, F), ("ij cj ya", 512, F), ("k4 hm ls", 96, F), ("acc cc", 160, F),
+        ("i256 wt r ep u uv wv", 256, F), ("r256 ee cs8", 256, B), ("s2 m2 e3b b2 x2 y2 dd td", 64, F), ("l", 528, F),
+        ("e cs t1 t2 t3 v1 v3 tt tu tv tw win", 32, F),
         ("ow", 32, "uint16"), ("og", 24, "uint16"), ("off", 256, "uint16"), ("p", 6144, F)):
     for _k in _names.split():
         SCRATCH[_k] = ("sbuf", [128, _w], _t)
 SCRATCH["ps"] = ("psum", [128, 4096], F)
-SEMAPHORES = ["lu", "lx0", "lx1", "lx2", "lx3", "lw", "gi", "v", "s", "pe", "it1", "it2", "st",
-              "asc", "aa", "aap", "ab", "abp", "ac", "loc"]
+SEMAPHORES = ["lu", "lx0", "lx1", "lx2", "lx3", "lw0", "lw1", "gi", "v", "s", "pe", "l1", "l2", "st",
+              "aa", "aap", "ab", "abp", "ac", "loc"] + ["a%d" % _s for _s in range(8)]
 
 ADD, SUB, MUL, MAX, MIN = AluOpType.add, AluOpType.subtract, AluOpType.mult, AluOpType.max, AluOpType.min
-GE, GT, EQ, AND = AluOpType.is_ge, AluOpType.is_gt, AluOpType.is_equal, AluOpType.bitwise_and
+GE, GT, EQ, NE, AND = AluOpType.is_ge, AluOpType.is_gt, AluOpType.is_equal, AluOpType.not_equal, AluOpType.bitwise_and
 COPY = ActivationFunctionType.Copy
 
 
@@ -54,21 +54,28 @@ def rank_program(g, core, T, topo):
             chips.append(topo.chip(c))
     on = lambda ch: [c for c in cores if topo.chip(c) == ch]
     mychip = topo.chip(core)
-    kind = on(mychip).index(core)
-    mate = [c for c in on(mychip) if c != core][0]
-    far = [c for c in cores if topo.chip(c) != mychip]
-    same = [on(ch)[kind] for ch in chips if ch != mychip]
+    kind_of = lambda c: on(topo.chip(c)).index(c)
+    kind = kind_of(core)
+    mate = on(mychip)[1 - kind]
+
+    def chips_from(c):
+        a = chips.index(topo.chip(c))
+        return sorted([chips[(a + d) % len(chips)] for d in range(1, len(chips))], key=lambda ch: topo.same_plane(ch, topo.chip(c)))
+
+    far_of = lambda c: [on(ch)[k] for ch in chips_from(c) for k in (kind_of(c), 1 - kind_of(c))]
+    far = far_of(core)
+    same = far[::2]
+    arrive = sorted(far, key=lambda c: far_of(c).index(core))
     slot = lambda frm, to: 192 * [ch for ch in chips if ch != topo.chip(to)].index(topo.chip(frm))
     eng_far = [e for e in topo.engines(core, mate) if all(e in topo.engines(core, c) for c in far)]
-    eng_near = [e for e in topo.engines(core, mate) if e not in eng_far][:4]
+    eng_near = [e for e in topo.engines(core, mate) if e not in eng_far]
     n_far, n_near = len(eng_far), len(eng_near)
+    near_a, near_b = eng_near[:n_near // 2], eng_near[n_near // 2:]
     did = lambda c: DstId(rid=topo.addr(c)[0], pnc=topo.addr(c)[1])
 
     def start_of(s):
         c = cores[s]
-        if c in (core, mate):
-            return 0 if c == core else 96
-        return 192 + slot(c, core) + (0 if c in same else 96)
+        return 96 * kind_of(c) + (0 if c in on(mychip) else 192 + slot(c, core))
 
     def send(*transfers):
         n["loc"] += sum(len(m) for m, _, _, _ in transfers)
@@ -107,24 +114,28 @@ def rank_program(g, core, T, topo):
     A.wait_ge(S.v, v_oz)
     s_zt = inc("s", A.activation(T.zt[:, :], T.uw[:, 0:64].indirect(T.oz[:, 0:35]), COPY))
 
+    px = 704 * kind
     for q in range(4):
         if q == 3:
             V.wait_ge(S.s, s_zt)
             vec(V.quantize_mx(T.cz[:, :], T.pz[:, :], T.zt[:, :]))
         V.wait_ge(S["lx%d" % q], 16)
-        v_x = vec(V.quantize_mx(T.cx[:, 128 * q:128 * q + 128], T.px[:, 128 * q:128 * q + 128], T.xs[:, 512 * q:512 * q + 512]))
+        v_x = vec(V.quantize_mx(T.cx[:, 128 * q:128 * q + 128], T.pa[:, px + 128 * q:px + 128 * q + 128], T.xs[:, 512 * q:512 * q + 512]))
         if q == 0:
             v_wz = vec(V.memset(T.wz[:, 2048:3072], 0.0))
     for q in range(4):
         a, b = 12 - 4 * q, 128 * q
         P.wait_ge(S.v, v_x if q == 3 else v_x - 1)
         k_sc = inc("pe", P.matmul_mx(T.ps[:, 3584:3712], T.cz[:, a:a + 128], T.pz[:, a:a + 128],
-                                     T.cx[:, b:b + 128], T.px[:, b:b + 128], q == 0, q == 3))
+                                     T.cx[:, b:b + 128], T.pa[:, px + b:px + b + 128], q == 0, q == 3))
 
-    Y.wait_ge(S.v, v_wz)
-    Y.wait_ge(S.s, s_wz)
-    for q in range(8):
-        Y.dma_start(T.wz[16 * q:16 * q + 16, 512 * q:512 * q + 512], T.w[16 * q:16 * q + 16, :]).then_inc(S.lw, 16)
+    for q, k in ((Y, 0), (A, 1)):
+        q.wait_ge(S.v, v_wz)
+        q.wait_ge(S.s, s_wz)
+        for t in range(4 * k, 4 * k + 4):
+            for a in range(4):
+                r = 16 * ((2 * a + t) % 8)
+                q.dma_start(T.wz[r:r + 16, 512 * t + 128 * a:512 * t + 128 * a + 128], T.w[r:r + 16, 128 * a:128 * a + 128]).then_inc(S["lw%d" % k], 16)
 
     V.wait_ge(S.pe, k_sc)
     me = bitrev(rank)
@@ -133,15 +144,15 @@ def rank_program(g, core, T, topo):
     vw(tt(T.sm[:, :], T.ps[:, 3584:3712], T.ms[:, :], MUL))
     vw(tt(T.s2[:, :], T.sm[:, 0:64], T.sm[:, 64:128], ADD))
     g.wait_ge(S.v, tt(own, T.s2[:, 0:32], T.s2[:, 32:64], ADD))
-    near2 = eng_near[:2]
-    send((eng_far, S.asc, own, [(c, own) for c in far]), (near2, S.asc, own, [(mate, own)]))
+    sem_of = lambda c: S["a%d" % cores.index(c)]
+    send((eng_far, sem_of(core), own, [(c, own) for c in far]), (eng_near, sem_of(core), own, [(mate, own)]))
 
-    vec(V.memset(T.h[:, 0:128], 0.0))
+    h0 = 128 * (1 - kind)
+    vec(V.memset(T.h[:, 384 * kind:384 * kind + 128], 0.0))
     V.wait_ge(S.gi, k_c)
     ts(T.c1[:, :], T.ic[:, :], T.fa[:, 1:2], SUB)
     ts(T.cj[:, :], T.ij[:, :], T.fa[:, 0:1], ADD)
-    ts(T.m4[:, :], T.k4[:, :], T.fa[:, 2:3], EQ)
-    ts(T.r4[:, :], T.k4[:, :], 1.0, MIN)
+    ts(T.hm[:, :], T.k4[:, :], T.fa[:, 2:3], NE, 4096.0, MUL)
     ts(T.r16[:, :], T.i16[:, :], 1.0, MIN)
     ts(T.r256[:, :], T.i256[:, :], 1.0, MIN)
     vec(V.memset(T.one[:, :], 1.0))
@@ -149,100 +160,115 @@ def rank_program(g, core, T, topo):
     for b in range(8):
         vec(V.memset(T.kc[:, b:b + 1], float(start_of(bitrev(b)) + 96)))
         vec(V.memset(T.wt[:, 32 * b:32 * b + 32], float(bitrev(b))))
-    V.wait_ge(S.lw, 128)
-    vec(V.quantize_mx(T.cw[:, 0:512], T.pw[:, 0:512], T.wz[:, 0:2048]))
-    vec(V.quantize_mx(T.cw[:, 512:1024], T.pw[:, 512:1024], T.wz[:, 2048:4096]))
+    for k in range(2):
+        V.wait_ge(S["lw%d" % k], 256)
+        vec(V.quantize_mx(T.cw[:, 512 * k:512 * k + 512], T.pw[:, 512 * k:512 * k + 512], T.wz[:, 2048 * k:2048 * k + 2048]))
 
-    V.wait_ge(S.asc, n_far * len(far) + len(near2))
-    vw(n["v"])
     half = lambda t, k: t[:, 32 * k:32 * k + 32]
-    two = lambda t, k: t[:, 64 * k:64 * k + 64]
-    lo, hi = me & 3, me & 1
-    v_m1 = tt(T.m1[:, :], R(0, 4), R(4, 4), MAX)
-    tt(T.e1[:, :], own, R(me ^ 4), GT if me & 4 else GE)
-    vw(v_m1)
-    v_m2 = tt(T.m2[:, :], T.m1[:, 0:64], T.m1[:, 64:128], MAX)
-    v_e2 = tt(T.e2[:, :], half(T.m1, lo), half(T.m1, lo ^ 2), GT if me & 2 else GE)
-    vw(v_m2)
-    tt(T.e3[:, :], half(T.m2, hi), half(T.m2, hi ^ 1), GT if me & 1 else GE)
-    vw(v_e2)
-    v_e12 = tt(T.e12[:, :], T.e1[:, :], T.e2[:, :], MUL)
-    tt(half(T.e3b, 0), half(T.m2, 0), half(T.m2, 1), GE)
-    vw(v_e12)
-    v_e = tt(T.e[:, :], T.e12[:, :], T.e3[:, :], MUL)
-    tt(half(T.e3b, 1), half(T.m2, 1), half(T.m2, 0), GT)
+    blk = lambda c: bitrev(cores.index(c))
+    beats = lambda k, c, other: tt(half(T.cc, k), own, other, GT if cores.index(c) < rank else GE)
+    m1 = lambda j: tt(half(T.m1, j), R(j), R(j + 4), MAX)
+    b1 = lambda j: tt(half(T.b1, j), R(j + 4), R(j), GT)
+    m2 = lambda j: tt(half(T.m2, j), half(T.m1, j), half(T.m1, j + 2), MAX)
+    b2 = lambda j: tt(half(T.b2, j), half(T.m1, j + 2), half(T.m1, j), GT)
+    vw(n["v"])
+    V.wait_ge(sem_of(mate), n_near)
+    beats(0, mate, R(blk(mate)))
+    m1(me & 3)
+    b1(me & 3)
+    so_far = half(T.cc, 0)
+    for k in (1, 2):
+        c = arrive[2 * k - 2]
+        j = blk(c) & 3
+        V.wait_ge(sem_of(c), n_far)
+        V.wait_ge(sem_of(arrive[2 * k - 1]), n_far)
+        v = m1(j)
+        b1(j)
+        vw(v)
+        vw(beats(k, c, half(T.m1, j)))
+        tt(half(T.acc, k), so_far, half(T.cc, k), MUL)
+        so_far = half(T.acc, k)
+    jz = blk(arrive[5]) & 3
+    m2(1 - (jz & 1))
+    b2(1 - (jz & 1))
+    V.wait_ge(sem_of(arrive[4]), n_far)
+    vw(beats(3, arrive[4], R(blk(arrive[4]))))
+    tt(half(T.acc, 3), so_far, half(T.cc, 3), MUL)
+    V.wait_ge(sem_of(arrive[5]), n_far)
+    v = beats(4, arrive[5], R(blk(arrive[5])))
+    m1(jz)
+    vw(v)
+    v_e = tt(T.e[:, :], half(T.acc, 3), half(T.cc, 4), MUL)
+    b1(jz)
     vw(v_e)
     v_cs = scan(T.cs[:, :], T.one[:, :], T.e[:, :], ADD, SUB)
-    v_v1 = tt(T.v1[:, :], T.e[:, :], T.c1[:, :], MUL)
+    tt(T.v1[:, :], T.e[:, :], T.c1[:, :], MUL)
     vw(v_cs)
     v_t1 = vec(V.transpose(T.t1[:, :], T.cs[:, :]))
-    vw(v_v1)
+    vw(v_t1 - 1)
     tt(T.v3[:, :], T.v1[:, :], T.cs[:, :], ADD)
     vw(v_t1)
     v_t2 = scan(T.t2[:, :], T.r16[:, :], T.t1[:, :])
-    v_b2 = tt(T.b2[:, :], T.m1[:, 64:128], T.m1[:, 0:64], GT)
+    m2(jz & 1)
     vw(v_t2)
     v_t3 = vec(V.transpose(T.t3[:, :], T.t2[:, :]))
-    vw(v_b2)
-    v_g2 = tt(T.g2[:, 64:128], T.e3b[:, :], T.b2[:, :], MUL)
+    b2(jz & 1)
     vw(v_t3)
     v_ow = ts(T.ow[:, :], T.v3[:, :], T.t3[:, 31:32], ADD, T.cs[:, 31:32], SUB)
-    vw(v_g2)
-    tt(T.g2[:, 0:64], T.e3b[:, :], T.g2[:, 64:128], SUB)
+    tt(half(T.e3b, 0), half(T.m2, 0), half(T.m2, 1), GE)
     vw(v_ow)
     v_l = vec(V.tensor_copy(T.l[:, 0:528].indirect(T.ow[:, 0:32]), T.cj[:, :]))
-    v_b1 = tt(T.b1[:, :], R(4, 4), R(0, 4), GT)
+    tt(half(T.e3b, 1), half(T.m2, 1), half(T.m2, 0), GT)
     vw(v_l)
-    v_lm = tt(T.lm[:, :], T.l[:, 417:513], T.m4[:, :], MUL)
-    vw(v_b1)
-    v_eh = tt(T.ee[:, 128:256], T.g2[:, :], T.b1[:, :], MUL)
-    vw(v_lm)
-    v_ls = scan(T.ls[:, :], T.r4[:, :], T.lm[:, :])
-    vw(v_eh)
-    v_ee = tt(T.ee[:, 0:128], T.g2[:, :], T.ee[:, 128:256], SUB)
-    A.wait_ge(S.v, v_ee)
-    s_ep = inc("s", A.activation(T.ep[:, :], T.ee[:, :], COPY))
+    v_ls = scan(T.ls[:, :], T.hm[:, :], T.l[:, 417:513], MIN, MAX)
+    vw(v_ls - 1)
+    tt(T.g2[:, 64:128], T.e3b[:, :], T.b2[:, :], MUL)
     vw(v_ls)
     v_og = vec(V.tensor_copy(T.og[:, :], T.ls[:, 3:96:4]))
     A.wait_ge(S.v, v_og)
-    s_h = inc("s", A.activation(T.h[:, 320:512], T.xs[:, 0:2048].indirect(T.og[:, 12:24]), COPY))
-    vw(v_ee)
-    v_cs8 = scan(T.cs8[:, :], T.r256[:, :], T.ee[:, :], MUL, SUB)
+    s_h = inc("s", A.activation(T.h[:, h0 + 192:h0 + 384], T.xs[:, 0:2048].indirect(T.og[:, 12:24]), COPY))
+    vw(v_og - 1)
+    tt(T.g2[:, 0:64], T.e3b[:, :], T.g2[:, 64:128], SUB)
     vw(v_og)
-    v_h = vec(V.tensor_copy(T.h[:, 128:320], T.xs[:, 0:2048].indirect(T.og[:, 0:12])))
-    vw(v_cs8)
-    v_tt = vec(V.tensor_copy(T.tt[:, 0:8], T.cs8[:, 31:256:32]))
+    v_h = vec(V.tensor_copy(T.h[:, h0:h0 + 192], T.xs[:, 0:2048].indirect(T.og[:, 0:12])))
     vw(v_h)
     V.wait_ge(S.s, s_h)
-    v_q = vec(V.quantize_mx(T.ca[:, 0:128], T.pa[:, 0:128], T.h[:, :]))
+    c0, cq = 32 + 96 * kind, 128 * kind
+    v_q = vec(V.quantize_mx(T.ca[:, cq:cq + 128], T.pa[:, 480 + cq:480 + cq + 128], T.h[:, :]))
     g.wait_ge(S.v, v_q)
-    by = lambda t, a: t[:, a:a + 96].bitcast(dt.uint8)
-    send((eng_far, S.ab, by(T.ca, 32), [(c, by(T.cb, slot(core, c))) for c in same]),
-         (eng_near, S.aa, by(T.ca, 32), [(mate, by(T.ca, 128))]))
-    send((eng_near, S.aap, T.pa[:, 32:128], [(mate, T.pa[:, 128:224])]))
+    by = lambda t, a, w=96: t[:, a:a + w].bitcast(dt.uint8)
+    wide = T.pa[:, 224 + 384 * kind:608 + 384 * kind]
+    send((eng_far, S.ab, by(T.ca, c0), [(c, by(T.cb, slot(core, c) + 96 * kind)) for c in same]), (eng_near, S.aap, wide, [(mate, wide)]))
     g.wait_ge(S.aap, n_near)
-    send((eng_far, S.abp, T.pa[:, 32:224], [(c, T.pb[:, slot(core, c):slot(core, c) + 192]) for c in same]))
+    send((eng_far, S.abp, T.pa[:, 512:704], [(c, T.pb[:, slot(core, c):slot(core, c) + 192]) for c in same]),
+         *[(m, S.aa, by(T.ca, c0 + a, 48), [(mate, by(T.ca, c0 + a, 48))]) for m, a in ((near_a, 0), (near_b, 48))])
     g.wait_ge(S.ab, n_far * len(same))
-    on_with = [eng_far[:n_far // 2], eng_far[n_far // 2:], eng_near]
-    send(*[(on_with[k], S.ac, by(T.cb, 192 * k), [(mate, by(T.cb, 192 * k + 96))]) for k in range(len(same))])
+    send(*[(m, S.ac, by(T.cb, 192 * k + 96 * kind), [(mate, by(T.cb, 192 * k + 96 * kind))]) for k, m in enumerate((near_a, near_b, eng_far))])
 
     freed = [None] * 8
 
-    def product(q, bank, codes, plane, a, w, skip, at):
+    def product(q, bank, codes, plane, w, skip, keep, at):
         if freed[bank]:
             P.wait_ge(S.s, freed[bank])
         c = 512 * bank
-        k = inc("pe", P.matmul_mx(T.ps[:, c:c + w], T.cw[:, 128 * q:128 * q + 128], T.pw[:, 128 * q:128 * q + 128],
-                                  codes[:, a:a + w], plane[:, a:a + w], True, True))
+        k = inc("pe", P.matmul_mx(T.ps[:, c:c + w], T.cw[:, 128 * q:128 * q + 128], T.pw[:, 128 * q:128 * q + 128], codes, plane, True, True))
         A.wait_ge(S.pe, k)
-        freed[bank] = inc("s", A.activation(T.p[:, 768 * q + at:768 * q + at + w - skip], T.ps[:, c + skip:c + w], COPY))
+        freed[bank] = inc("s", A.activation(T.p[:, 768 * q + at:768 * q + at + keep], T.ps[:, c + skip:c + skip + keep], COPY))
         return freed[bank]
 
-    P.wait_ge(S.v, v_q)
-    for q in range(8):
-        product(q, q, T.ca, T.pa, 0, 128, 32, 0)
+    def pair(a, skip, at):
+        for q in range(8):
+            product(q, q, T.ca[:, a:a + 128], T.pa[:, 480 + a:480 + a + 128], 128, skip, 96, at)
 
-    vw(v_tt)
+    vw(tt(T.ee[:, 128:256], T.g2[:, :], T.b1[:, :], MUL))
+    v_ee = tt(T.ee[:, 0:128], T.g2[:, :], T.ee[:, 128:256], SUB)
+    A.wait_ge(S.v, v_ee)
+    s_ep = inc("s", A.activation(T.ep[:, :], T.ee[:, :], COPY))
+    P.wait_ge(S.v, v_q)
+    pair(cq, c0 - cq, 96 * kind)
+    vw(v_ee)
+    vw(scan(T.cs8[:, :], T.r256[:, :], T.ee[:, :], MUL, SUB))
+    vw(vec(V.tensor_copy(T.tt[:, 0:8], T.cs8[:, 31:256:32])))
     v_tu = vec(V.transpose(T.tu[:, :], T.tt[:, :]))
     tt(T.st1[:, :], T.kc[:, :], T.tt[:, 0:8], SUB)
     vw(v_tu)
@@ -255,36 +281,42 @@ def rank_program(g, core, T, topo):
     vw(tt(T.uv[:, :], T.u[:, :], T.ee[:, :], MUL))
     vw(tt(T.x1[:, :], T.uv[:, 0:128], T.uv[:, 128:256], ADD))
     vw(tt(T.x2[:, :], T.x1[:, 0:64], T.x1[:, 64:128], ADD))
-    vw(tt(T.ix[:, :], T.x2[:, 0:32], T.x2[:, 32:64], ADD))
-    v_it = vec(V.transpose(T.it[:, :], T.ix[:, :]))
-    for q, b in ((Y, 0), (A, 1)):
-        q.wait_ge(S.v, v_it)
-        for k in range(4):
-            q.dma_start(T.bx[0:16, 128 * b + 32 * k:128 * b + 32 * k + 32], T.it[32 * k + 16 * b:32 * k + 16 * b + 16, :]).then_inc(S.it1, 16)
-    Y.wait_ge(S.it1, 128)
-    for q in range(1, 8):
-        Y.dma_start(T.bx[16 * q:16 * q + 16, :], T.bx[0:16, :]).then_inc(S.it2, 16)
+    for k in range(4):
+        a = 16 * (k // 2)
+        v = tt(T.dd[:, 16 * k:16 * k + 16], T.x2[:, a:a + 16], T.x2[:, 32 + a:48 + a], ADD)
+    vw(v)
+    vw(vec(V.transpose(T.td[:, :], T.dd[:, :])))
+    vec(V.tensor_copy(T.off[:, 0:64:2], T.td[:, 0:32]))
+    v_off = vec(V.tensor_copy(T.off[:, 1:64:2], T.td[:, 32:64]))
+
+    def turn(k, sem):
+        Y.dma_start(T.off[0:128 - 32 * k, 64 * k:64 * k + 64], T.off[32 * k:128, 0:64]).then_inc(sem, 16)
+        Y.dma_start(T.off[128 - 32 * k:128, 64 * k:64 * k + 64], T.off[0:32 * k, 0:64]).then_inc(sem, 16)
+
+    Y.wait_ge(S.v, v_off)
+    turn(1, S.l1)
     vw(tt(T.wv[:, :], T.ee[:, :], T.wt[:, :], MUL))
     vw(tt(T.y1[:, :], T.wv[:, 0:128], T.wv[:, 128:256], ADD))
     vw(tt(T.y2[:, :], T.y1[:, 0:64], T.y1[:, 64:128], ADD))
-    Y.wait_ge(S.v, tt(T.win[:, :], T.y2[:, 0:32], T.y2[:, 32:64], ADD))
-    Y.dma_start(T.wn[:, :], T.win[:, :]).then_inc(S.st, 16)
+    v_win = tt(T.win[:, :], T.y2[:, 0:32], T.y2[:, 32:64], ADD)
 
     P.wait_ge(S.aap, n_near)
     P.wait_ge(S.aa, n_near)
-    for q in range(8):
-        product(q, q, T.ca, T.pa, 96, 128, 32, 96)
-    V.wait_ge(S.it1, 128)
-    V.wait_ge(S.it2, 112)
-    vec(V.tensor_copy(T.off[:, 0:256:2], T.bx[:, 0:128]))
-    v_off = vec(V.tensor_copy(T.off[:, 1:256:2], T.bx[:, 128:256]))
+    pair(96 - 64 * kind, 32 - 32 * kind, 96 - 96 * kind)
+    Y.wait_ge(S.ac, n_far + n_near)
+    turn(2, S.l2)
+    turn(3, S.l2)
+    Y.wait_ge(S.v, v_win)
+    Y.dma_start(T.wn[:, :], T.win[:, :]).then_inc(S.st, 16)
     pick_of = lambda q, a, b: T.p[:, 768 * q:768 * q + 768].indirect(T.off[:, 32 * q + a // 16:32 * q + b // 16])
     P.wait_ge(S.ab, n_far * len(same))
     P.wait_ge(S.abp, n_far * len(same))
     P.wait_ge(S.ac, n_far + n_near)
     ready = []
     for q in range(8):
-        ready.append([product(q, (2 * q + k) % 8, T.cb, T.pb, 288 * k, 288, 0, 192 + 288 * k) for k in range(2)][1])
+        for k in range(2):
+            done = product(q, (2 * q + k) % 8, T.cb[:, 288 * k:288 * k + 288], T.pb[:, 288 * k:288 * k + 288], 288, 0, 288, 192 + 288 * k)
+        ready.append(done)
         if q == 1:
             A.wait_ge(S.v, v_off)
             A.wait_ge(S.s, ready[0])
@@ -303,6 +335,8 @@ def rank_program(g, core, T, topo):
     V.wait_ge(S.s, s_half)
     last = pick(1, 256, 512, last)
     for q in range(2, 6):
+        if q in (2, 4):
+            V.wait_ge(*((S.l1, 32) if q == 2 else (S.l2, 64)))
         last = pick(q, 0, 512, last)
     for a in (0, 256):
         k = pick(7, a, a + 256, pick(6, a, a + 256, last))

@@ -5,18 +5,19 @@ F4, F, B = "float8_e4m3fn_x4", "float32", "bfloat16"
 SCRATCH = {}
 for _names, _w, _t in (
         ("uw", 64, B), ("xs", 2048, B), ("zt", 560, B), ("wz", 4096, B), ("h", 512, B),
-        ("cz", 140, F4), ("pz", 140, "uint8"), ("cx", 512, F4), ("cw", 1024, F4), ("pw", 1024, "uint8"),
-        ("ca", 256, F4), ("pa", 1216, "uint8"), ("cb", 576, F4), ("pb", 576, "uint8"),
-        ("ia ib", 4, "int32"), ("fa", 4, F), ("g8 kc st1 st2", 8, F), ("v32 ms sm m1 b1 g2 x1 y1", 128, F),
-        ("oz", 36, "uint16"), ("ic c1 i16 r16 one", 32, F), ("ij cj ya", 512, F), ("k4 hm ls", 96, F), ("acc cc", 160, F),
-        ("i256 wt r ep u uv wv", 256, F), ("r256 ee cs8", 256, B), ("s2 m2 e3b b2 x2 y2 dd td", 64, F), ("l", 528, F),
-        ("e cs t1 t2 t3 v1 v3 tt tu tv tw win", 32, F),
+        ("cz", 140, F4), ("pz", 140, "uint8"), ("cx", 256, F4), ("cw", 1024, F4), ("pw", 1024, "uint8"),
+        ("ca", 256, F4), ("pa", 992, "uint8"), ("cb", 640, F4), ("pb", 640, "uint8"),
+        ("ia ib", 8, "int32"), ("fa g8", 8, F), ("kc st1 st2 h4", 4, F),
+        ("v32 ms sm m1 b0 b1 g2 r128 ee cs4 u uv", 128, F), ("xi xj", 32, "int32"),
+        ("oz", 36, "uint16"), ("ic c1 r16 one", 32, F), ("cj ya", 512, F), ("hm ls", 96, F), ("acc cc", 224, F),
+        ("r", 256, F), ("s2 m2 e3b b2 x1 z1 dd td", 64, F), ("l", 528, F),
+        ("cs t1 t2 t3 v1 v3 tt tu tv tw x2 z sh y1 y2 y3 y4 y5 win", 32, F),
         ("ow", 32, "uint16"), ("og", 24, "uint16"), ("off", 256, "uint16"), ("p", 6144, F)):
     for _k in _names.split():
         SCRATCH[_k] = ("sbuf", [128, _w], _t)
 SCRATCH["ps"] = ("psum", [128, 4096], F)
-SEMAPHORES = ["lu", "lx0", "lx1", "lx2", "lx3", "lw0", "lw1", "gi", "v", "s", "pe", "l1", "l2", "st",
-              "aa", "aap", "ab", "abp", "ac", "loc"] + ["a%d" % _s for _s in range(8)]
+SEMAPHORES = ["lu", "lx0", "lx1", "lx2", "lw0", "lw1", "lw2", "lw3", "gi", "v", "s", "pe", "l1", "l2", "st",
+              "aa", "aap", "abp", "ac", "loc"] + ["%s%d" % (_k, _s) for _k in "ab" for _s in range(8)]
 
 ADD, SUB, MUL, MAX, MIN = AluOpType.add, AluOpType.subtract, AluOpType.mult, AluOpType.max, AluOpType.min
 GE, GT, EQ, NE, AND = AluOpType.is_ge, AluOpType.is_gt, AluOpType.is_equal, AluOpType.not_equal, AluOpType.bitwise_and
@@ -66,7 +67,15 @@ def rank_program(g, core, T, topo):
     far = far_of(core)
     same = far[::2]
     arrive = sorted(far, key=lambda c: far_of(c).index(core))
-    slot = lambda frm, to: 192 * [ch for ch in chips if ch != topo.chip(to)].index(topo.chip(frm))
+    flip = lambda ch: chips.index(ch) // 2
+    pos_of = lambda c: kind_of(c) ^ flip(topo.chip(c))
+    pos = pos_of(core)
+
+    def slot(frm, to):
+        a, b, c = sorted([ch for ch in chips if ch != topo.chip(to)], key=lambda ch: flip(ch) == flip(topo.chip(to)))
+        return 32 + 192 * [a, c, b].index(topo.chip(frm))
+
+    col = lambda c, to=core: slot(c, to) + 96 * pos_of(c)
     eng_far = [e for e in topo.engines(core, mate) if all(e in topo.engines(core, c) for c in far)]
     eng_near = [e for e in topo.engines(core, mate) if e not in eng_far]
     n_far, n_near = len(eng_far), len(eng_near)
@@ -75,7 +84,7 @@ def rank_program(g, core, T, topo):
 
     def start_of(s):
         c = cores[s]
-        return 96 * kind_of(c) + (0 if c in on(mychip) else 192 + slot(c, core))
+        return 96 * pos_of(c) if c in on(mychip) else 160 + col(c)
 
     def send(*transfers):
         n["loc"] += sum(len(m) for m, _, _, _ in transfers)
@@ -83,59 +92,71 @@ def rank_program(g, core, T, topo):
                                               srcs=[src], dsts=[d for _, d in to], alu_op=0) for m, sem, src, to in transfers], local_sem=S.loc)
 
     Y.dma_start(T.uw[:, 0:64], T.us[:, 0:64]).then_inc(S.lu, 16)
-    for q, k in ((A, 0), (Y, 1), (A, 2), (Y, 3)):
-        q.dma_start(T.xs[:, 512 * k:512 * k + 512], T.x[:, 512 * k:512 * k + 512]).then_inc(S["lx%d" % k], 16)
+    for k, (q, a, b) in enumerate(((A, 0, 1024), (Y, 1024, 1536), (A, 1536, 2048))):
+        q.dma_start(T.xs[:, a:b], T.x[:, a:b]).then_inc(S["lx%d" % k], 16)
 
-    inc("gi", g.iota(T.ia[:, 0:1], [[0, 1]], 0, 1))
-    inc("gi", g.iota(T.ia[:, 1:2], [[0, 1]], 0, 32))
+    k_p = inc("gi", g.iota(T.ia[:, 0:1], [[0, 1]], 0, 1))
     k_a = iota(T.g8[:, :], [[4, 8]], 0, 0)
     k_b = iota(T.v32[:, :], [[1, 4], [0, 32]], 0, 0)
     iota(T.ic[:, :], [[-1, 32]], 512, 0)
-    iota(T.k4[:, :], [[0, 24], [1, 4]], 0, 0)
-    iota(T.i16[:, :], [[0, 2], [1, 16]], 0, 0)
-    iota(T.ij[:, :], [[4, 32], [128, 16]], 0, 0)
-    k_c = iota(T.i256[:, :], [[0, 8], [1, 32]], 0, 0)
+    k_c = iota(T.cj[:, :], [[4, 32], [128, 16]], 0, 0)
+
+    def load_w(k):
+        for t in (2 * k, 2 * k + 1):
+            for a in range(4):
+                r = 16 * ((2 * a + t) % 8)
+                Y.dma_start(T.wz[r:r + 16, 512 * t + 128 * a:512 * t + 128 * a + 128], T.w[r:r + 16, 128 * a:128 * a + 128]).then_inc(S["lw%d" % k], 16)
+
+    def zeros(k):
+        Y.wait_ge(S.v, vec(V.memset(T.wz[:, 1024 * k:1024 * k + 1024], 0.0)))
+
+    def pack(k):
+        V.wait_ge(S["lw%d" % k], 128)
+        return vec(V.quantize_mx(T.cw[:, 256 * k:256 * k + 256], T.pw[:, 256 * k:256 * k + 256], T.wz[:, 1024 * k:1024 * k + 1024]))
 
     vec(V.memset(T.oz[:, :], 32))
-    v_z = vec(V.memset(T.wz[:, 0:1024], 0.0))
-    A.wait_ge(S.v, v_z)
-    s_wz = inc("s", A.activation(T.wz[:, 3072:4096], T.wz[:, 0:1024], COPY))
+    zeros(3)
+    A.wait_ge(S.v, n["v"])
+    Y.wait_ge(S.s, inc("s", A.activation(T.wz[:, 0:1024], T.wz[:, 3072:4096], COPY)))
     V.wait_ge(S.gi, k_a)
     ts(T.ib[:, 0:1], T.ia[:, 0:1], 3, AND)
-    ts(T.ib[:, 1:2], T.ia[:, 1:2], 511, AND)
+    ts(T.ib[:, 1:2], T.ia[:, 0:1], 15, AND)
     vw(ts(T.ib[:, 2:3], T.ia[:, 0:1], 12, AND, 2, AluOpType.arith_shift_right))
     vw(vec(V.tensor_copy(T.fa[:, 0:3], T.ib[:, 0:3])))
     v_oz = ts(T.oz[:, 3:32:4], T.g8[:, :], T.fa[:, 0:1], ADD)
-    vec(V.memset(T.wz[:, 1024:2048], 0.0))
+    ts(T.fa[:, 4:5], T.fa[:, 1:2], 32.0, MUL)
+    load_w(0)
+    zeros(1)
+    load_w(1)
     V.wait_ge(S.gi, k_b)
     ts(T.ms[:, :], T.v32[:, :], T.fa[:, 0:1], EQ)
+    zeros(2)
+    load_w(2)
+    load_w(3)
 
     A.wait_ge(S.lu, 16)
     A.wait_ge(S.v, v_oz)
-    s_zt = inc("s", A.activation(T.zt[:, :], T.uw[:, 0:64].indirect(T.oz[:, 0:35]), COPY))
+    s_zt = inc("s", A.activation(T.zt[:, 0:320], T.uw[:, 0:64].indirect(T.oz[:, 0:20]), COPY))
+    V.wait_ge(S.lu, 16)
+    vw(v_oz)
+    v_zt = vec(V.tensor_copy(T.zt[:, 320:560], T.uw[:, 0:64].indirect(T.oz[:, 20:35])))
 
-    px = 704 * kind
+    px = 224 + 512 * pos
+    quarter = [(T.cb[:, 0:128], T.pb[:, 0:128]), (T.cb[:, 512:640], T.pb[:, 512:640]),
+               (T.cx[:, 0:128], T.pa[:, px:px + 128]), (T.cx[:, 128:256], T.pa[:, px + 128:px + 256])]
+    v_x = []
     for q in range(4):
-        if q == 3:
+        if q == 2:
             V.wait_ge(S.s, s_zt)
-            vec(V.quantize_mx(T.cz[:, :], T.pz[:, :], T.zt[:, :]))
-        V.wait_ge(S["lx%d" % q], 16)
-        v_x = vec(V.quantize_mx(T.cx[:, 128 * q:128 * q + 128], T.pa[:, px + 128 * q:px + 128 * q + 128], T.xs[:, 512 * q:512 * q + 512]))
-        if q == 0:
-            v_wz = vec(V.memset(T.wz[:, 2048:3072], 0.0))
+            vw(v_zt)
+            v_cz = vec(V.quantize_mx(T.cz[:, :], T.pz[:, :], T.zt[:, :]))
+        if q != 1:
+            V.wait_ge(S["lx%d" % max(q - 1, 0)], 16)
+        v_x.append(vec(V.quantize_mx(*quarter[q], T.xs[:, 512 * q:512 * q + 512])))
     for q in range(4):
-        a, b = 12 - 4 * q, 128 * q
-        P.wait_ge(S.v, v_x if q == 3 else v_x - 1)
-        k_sc = inc("pe", P.matmul_mx(T.ps[:, 3584:3712], T.cz[:, a:a + 128], T.pz[:, a:a + 128],
-                                     T.cx[:, b:b + 128], T.pa[:, px + b:px + b + 128], q == 0, q == 3))
-
-    for q, k in ((Y, 0), (A, 1)):
-        q.wait_ge(S.v, v_wz)
-        q.wait_ge(S.s, s_wz)
-        for t in range(4 * k, 4 * k + 4):
-            for a in range(4):
-                r = 16 * ((2 * a + t) % 8)
-                q.dma_start(T.wz[r:r + 16, 512 * t + 128 * a:512 * t + 128 * a + 128], T.w[r:r + 16, 128 * a:128 * a + 128]).then_inc(S["lw%d" % k], 16)
+        a = 12 - 4 * q
+        P.wait_ge(S.v, max(v_x[q], v_cz))
+        k_sc = inc("pe", P.matmul_mx(T.ps[:, 3584:3712], T.cz[:, a:a + 128], T.pz[:, a:a + 128], *quarter[q], q == 0, q == 3))
 
     V.wait_ge(S.pe, k_sc)
     me = bitrev(rank)
@@ -145,64 +166,55 @@ def rank_program(g, core, T, topo):
     vw(tt(T.s2[:, :], T.sm[:, 0:64], T.sm[:, 64:128], ADD))
     g.wait_ge(S.v, tt(own, T.s2[:, 0:32], T.s2[:, 32:64], ADD))
     sem_of = lambda c: S["a%d" % cores.index(c)]
-    send((eng_far, sem_of(core), own, [(c, own) for c in far]), (eng_near, sem_of(core), own, [(mate, own)]))
+    send((eng_far, sem_of(core), own, [(c, own) for c in far]))
+    send((eng_near, sem_of(core), own, [(mate, own)]))
 
-    h0 = 128 * (1 - kind)
-    vec(V.memset(T.h[:, 384 * kind:384 * kind + 128], 0.0))
+    h0 = 128 * (1 - pos)
+    vec(V.memset(T.h[:, 384 * pos:384 * pos + 128], 0.0))
     V.wait_ge(S.gi, k_c)
-    ts(T.c1[:, :], T.ic[:, :], T.fa[:, 1:2], SUB)
-    ts(T.cj[:, :], T.ij[:, :], T.fa[:, 0:1], ADD)
-    ts(T.hm[:, :], T.k4[:, :], T.fa[:, 2:3], NE, 4096.0, MUL)
-    ts(T.r16[:, :], T.i16[:, :], 1.0, MIN)
-    ts(T.r256[:, :], T.i256[:, :], 1.0, MIN)
-    vec(V.memset(T.one[:, :], 1.0))
+    ts(T.c1[:, :], T.ic[:, :], T.fa[:, 4:5], SUB)
+    ts(T.h4[:, :], T.v32[:, 0:128:32], T.fa[:, 2:3], NE, 4096.0, MUL)
+    for t in (T.one, T.r16, T.r128):
+        v = vec(V.memset(t[:, :], 1.0))
+    vw(v)
+    for k in range(4):
+        ts(T.hm[:, k:96:4], T.one[:, 0:24], T.h4[:, k:k + 1], MUL)
+    vec(V.memset(T.r16[:, 0:32:16], 0.0))
+    vec(V.memset(T.r128[:, 0:128:32], 0.0))
     vec(V.memset(T.tt[:, :], 0.0))
-    for b in range(8):
-        vec(V.memset(T.kc[:, b:b + 1], float(start_of(bitrev(b)) + 96)))
-        vec(V.memset(T.wt[:, 32 * b:32 * b + 32], float(bitrev(b))))
-    for k in range(2):
-        V.wait_ge(S["lw%d" % k], 256)
-        vec(V.quantize_mx(T.cw[:, 512 * k:512 * k + 512], T.pw[:, 512 * k:512 * k + 512], T.wz[:, 2048 * k:2048 * k + 2048]))
+    for b in range(4):
+        vec(V.memset(T.kc[:, b:b + 1], float(start_of(bitrev(b)) + 96 + 2048 * (start_of(bitrev(b + 4)) + 96))))
+    pack(0)
+    pack(1)
 
     half = lambda t, k: t[:, 32 * k:32 * k + 32]
     blk = lambda c: bitrev(cores.index(c))
     beats = lambda k, c, other: tt(half(T.cc, k), own, other, GT if cores.index(c) < rank else GE)
     m1 = lambda j: tt(half(T.m1, j), R(j), R(j + 4), MAX)
-    b1 = lambda j: tt(half(T.b1, j), R(j + 4), R(j), GT)
+    b0 = lambda j: tt(half(T.b0, j), R(j + 4), R(j), GT)
+    b1 = lambda j: ts(half(T.b1, j), half(T.b0, j), 2047.0, MUL, 1.0, ADD)
     m2 = lambda j: tt(half(T.m2, j), half(T.m1, j), half(T.m1, j + 2), MAX)
     b2 = lambda j: tt(half(T.b2, j), half(T.m1, j + 2), half(T.m1, j), GT)
+    j0, jx, jy, jz = me & 3, blk(arrive[1]) & 3, blk(arrive[3]) & 3, blk(arrive[5]) & 3
+    beside = [[], [(m1, jx), (b0, jx)], [(b1, jx)], [(m1, j0), (b0, j0)], [(b1, j0), (m1, jy)], [(b0, jy)], [(m1, jz)]]
     vw(n["v"])
-    V.wait_ge(sem_of(mate), n_near)
-    beats(0, mate, R(blk(mate)))
-    m1(me & 3)
-    b1(me & 3)
-    so_far = half(T.cc, 0)
-    for k in (1, 2):
-        c = arrive[2 * k - 2]
-        j = blk(c) & 3
-        V.wait_ge(sem_of(c), n_far)
-        V.wait_ge(sem_of(arrive[2 * k - 1]), n_far)
-        v = m1(j)
-        b1(j)
-        vw(v)
-        vw(beats(k, c, half(T.m1, j)))
-        tt(half(T.acc, k), so_far, half(T.cc, k), MUL)
-        so_far = half(T.acc, k)
-    jz = blk(arrive[5]) & 3
+    for k, c in enumerate(arrive[:3] + [mate] + arrive[3:]):
+        V.wait_ge(sem_of(c), n_near if c == mate else n_far)
+        v = beats(k, c, R(blk(c)))
+        vw(v - 1)
+        for call, j in beside[k]:
+            call(j)
+        if k:
+            vw(v)
+            v_e = tt(half(T.acc, k), so_far, half(T.cc, k), MUL)
+        else:
+            pack(2)
+        so_far = half(T.acc if k else T.cc, k)
+    e = so_far
     m2(1 - (jz & 1))
-    b2(1 - (jz & 1))
-    V.wait_ge(sem_of(arrive[4]), n_far)
-    vw(beats(3, arrive[4], R(blk(arrive[4]))))
-    tt(half(T.acc, 3), so_far, half(T.cc, 3), MUL)
-    V.wait_ge(sem_of(arrive[5]), n_far)
-    v = beats(4, arrive[5], R(blk(arrive[5])))
-    m1(jz)
-    vw(v)
-    v_e = tt(T.e[:, :], half(T.acc, 3), half(T.cc, 4), MUL)
-    b1(jz)
     vw(v_e)
-    v_cs = scan(T.cs[:, :], T.one[:, :], T.e[:, :], ADD, SUB)
-    tt(T.v1[:, :], T.e[:, :], T.c1[:, :], MUL)
+    v_cs = scan(T.cs[:, :], T.one[:, :], e, ADD, SUB)
+    tt(T.v1[:, :], e, T.c1[:, :], MUL)
     vw(v_cs)
     v_t1 = vec(V.transpose(T.t1[:, :], T.cs[:, :]))
     vw(v_t1 - 1)
@@ -221,71 +233,115 @@ def rank_program(g, core, T, topo):
     tt(half(T.e3b, 1), half(T.m2, 1), half(T.m2, 0), GT)
     vw(v_l)
     v_ls = scan(T.ls[:, :], T.hm[:, :], T.l[:, 417:513], MIN, MAX)
-    vw(v_ls - 1)
-    tt(T.g2[:, 64:128], T.e3b[:, :], T.b2[:, :], MUL)
+    b2(1 - (jz & 1))
     vw(v_ls)
-    v_og = vec(V.tensor_copy(T.og[:, :], T.ls[:, 3:96:4]))
+    v_og = ts(T.og[:, :], T.ls[:, 3:96:4], T.fa[:, 0:1], ADD)
     A.wait_ge(S.v, v_og)
     s_h = inc("s", A.activation(T.h[:, h0 + 192:h0 + 384], T.xs[:, 0:2048].indirect(T.og[:, 12:24]), COPY))
-    vw(v_og - 1)
-    tt(T.g2[:, 0:64], T.e3b[:, :], T.g2[:, 64:128], SUB)
+    b0(jz)
     vw(v_og)
     v_h = vec(V.tensor_copy(T.h[:, h0:h0 + 192], T.xs[:, 0:2048].indirect(T.og[:, 0:12])))
+    tt(half(T.g2, 2), half(T.e3b, 0), half(T.b2, 0), MUL)
     vw(v_h)
     V.wait_ge(S.s, s_h)
-    c0, cq = 32 + 96 * kind, 128 * kind
+    c0, cq = 32 + 96 * pos, 128 * pos
     v_q = vec(V.quantize_mx(T.ca[:, cq:cq + 128], T.pa[:, 480 + cq:480 + cq + 128], T.h[:, :]))
     g.wait_ge(S.v, v_q)
     by = lambda t, a, w=96: t[:, a:a + w].bitcast(dt.uint8)
-    wide = T.pa[:, 224 + 384 * kind:608 + 384 * kind]
-    send((eng_far, S.ab, by(T.ca, c0), [(c, by(T.cb, slot(core, c) + 96 * kind)) for c in same]), (eng_near, S.aap, wide, [(mate, wide)]))
+    wide = T.pa[:, 224 + 384 * pos:608 + 384 * pos]
+    codes_of = lambda c: S["b%d" % cores.index(c)]
+    send((eng_far, codes_of(core), by(T.ca, c0), [(c, by(T.cb, col(core, c))) for c in same]), (eng_near, S.aap, wide, [(mate, wide)]))
     g.wait_ge(S.aap, n_near)
     send((eng_far, S.abp, T.pa[:, 512:704], [(c, T.pb[:, slot(core, c):slot(core, c) + 192]) for c in same]),
          *[(m, S.aa, by(T.ca, c0 + a, 48), [(mate, by(T.ca, c0 + a, 48))]) for m, a in ((near_a, 0), (near_b, 48))])
-    g.wait_ge(S.ab, n_far * len(same))
-    send(*[(m, S.ac, by(T.cb, 192 * k + 96 * kind), [(mate, by(T.cb, 192 * k + 96 * kind))]) for k, m in enumerate((near_a, near_b, eng_far))])
+    direct = arrive[::2]
+    n_ac = 0
+    for step in (((direct[0], eng_near),), ((direct[1], eng_near), (direct[2], eng_far))):
+        for c, m in step:
+            g.wait_ge(codes_of(c), n_far)
+            n_ac += len(m)
+        send(*[(m, S.ac, by(T.cb, col(c)), [(mate, by(T.cb, col(c)))]) for c, m in step])
 
     freed = [None] * 8
+    bank = [0]
 
-    def product(q, bank, codes, plane, w, skip, keep, at):
-        if freed[bank]:
-            P.wait_ge(S.s, freed[bank])
-        c = 512 * bank
-        k = inc("pe", P.matmul_mx(T.ps[:, c:c + w], T.cw[:, 128 * q:128 * q + 128], T.pw[:, 128 * q:128 * q + 128], codes, plane, True, True))
-        A.wait_ge(S.pe, k)
-        freed[bank] = inc("s", A.activation(T.p[:, 768 * q + at:768 * q + at + keep], T.ps[:, c + skip:c + skip + keep], COPY))
-        return freed[bank]
+    def product(q, codes, plane, a, w, skip, keep, at, by_vector=False):
+        b = bank[0]
+        bank[0] = (b + 1) % 8
+        if freed[b]:
+            P.wait_ge(*freed[b])
+        c = 512 * b
+        k = inc("pe", P.matmul_mx(T.ps[:, c:c + w], T.cw[:, 128 * q:128 * q + 128], T.pw[:, 128 * q:128 * q + 128],
+                                  codes[:, a:a + w], plane[0][:, plane[1] + a:plane[1] + a + w], True, True))
+        out, res = T.p[:, 768 * q + at:768 * q + at + keep], T.ps[:, c + skip:c + skip + keep]
+        (V if by_vector else A).wait_ge(S.pe, k)
+        freed[b] = (S.v, vec(V.tensor_copy(out, res))) if by_vector else (S.s, inc("s", A.activation(out, res, COPY)))
+        return freed[b]
 
-    def pair(a, skip, at):
-        for q in range(8):
-            product(q, q, T.ca[:, a:a + 128], T.pa[:, 480 + a:480 + a + 128], 128, skip, 96, at)
+    def pair(a, skip, at, tiles, by_vector=False):
+        for q in tiles:
+            product(q, T.ca, (T.pa, 480), a, 128, skip, 96, at, by_vector)
 
-    vw(tt(T.ee[:, 128:256], T.g2[:, :], T.b1[:, :], MUL))
-    v_ee = tt(T.ee[:, 0:128], T.g2[:, :], T.ee[:, 128:256], SUB)
-    A.wait_ge(S.v, v_ee)
-    s_ep = inc("s", A.activation(T.ep[:, :], T.ee[:, :], COPY))
-    P.wait_ge(S.v, v_q)
-    pair(cq, c0 - cq, 96 * kind)
-    vw(v_ee)
-    vw(scan(T.cs8[:, :], T.r256[:, :], T.ee[:, :], MUL, SUB))
-    vw(vec(V.tensor_copy(T.tt[:, 0:8], T.cs8[:, 31:256:32])))
-    v_tu = vec(V.transpose(T.tu[:, :], T.tt[:, :]))
-    tt(T.st1[:, :], T.kc[:, :], T.tt[:, 0:8], SUB)
-    vw(v_tu)
-    vw(scan(T.tv[:, :], T.r16[:, :], T.tu[:, :]))
-    vw(vec(V.transpose(T.tw[:, :], T.tv[:, :])))
-    vw(tt(T.st2[:, :], T.st1[:, :], T.tw[:, 0:8], ADD))
-    V.wait_ge(S.s, s_ep)
-    vw(tt(T.ep[:, 0:256:32], T.ep[:, 0:256:32], T.st2[:, :], SUB))
-    vw(scan(T.u[:, :], T.r256[:, :], T.ep[:, :], MUL, SUB))
-    vw(tt(T.uv[:, :], T.u[:, :], T.ee[:, :], MUL))
-    vw(tt(T.x1[:, :], T.uv[:, 0:128], T.uv[:, 128:256], ADD))
-    vw(tt(T.x2[:, :], T.x1[:, 0:64], T.x1[:, 64:128], ADD))
+    def three(q, blocks, two_by_vector, one_by_vector):
+        a, b, c = sorted(col(x) for x in blocks)
+        two, one = (a, c) if b == a + 96 else (b, a)
+        skip = 32 if one == 32 else 0
+        return [product(q, T.cb, (T.pb, 0), two, 192, 0, 192, 160 + two, two_by_vector),
+                product(q, T.cb, (T.pb, 0), one - skip, 128, skip, 96, 160 + one, one_by_vector)]
+
+    P.wait_ge(S.v, pack(3))
+    pair(cq, c0 - cq, 96 * pos, range(8))
+
+    def chain(links, beside):
+        v = n["v"]
+        for k, link in enumerate(links):
+            vw(v)
+            v = link()
+            if k < len(beside) and beside[k]:
+                beside[k]()
+        return v
+
+    v = tt(half(T.g2, 3), half(T.e3b, 1), half(T.b2, 1), MUL)
+    b1(jy)
+    b1(jz)
+    vw(v)
+    tt(T.g2[:, 0:64], T.e3b[:, :], T.g2[:, 64:128], SUB)
+    v = chain([
+        lambda: tt(T.ee[:, :], T.g2[:, :], T.b1[:, :], MUL),
+        lambda: scan(T.cs4[:, :], T.r128[:, :], T.ee[:, :], MUL, SUB),
+        lambda: vec(V.tensor_copy(T.tt[:, 0:4], T.cs4[:, 31:128:32])),
+        lambda: vec(V.transpose(T.tu[:, :], T.tt[:, :])),
+        lambda: scan(T.tv[:, :], T.r16[:, :], T.tu[:, :]),
+        lambda: vec(V.transpose(T.tw[:, :], T.tv[:, :])),
+        lambda: tt(T.ee[:, 0:128:32], T.st2[:, :], T.tw[:, 0:4], SUB),
+        lambda: scan(T.u[:, :], T.r128[:, :], T.ee[:, :], MUL, SUB),
+        lambda: tt(T.uv[:, :], T.u[:, :], T.g2[:, :], MUL),
+        lambda: tt(T.x1[:, :], T.uv[:, 0:64], T.uv[:, 64:128], ADD),
+        lambda: tt(T.x2[:, :], T.x1[:, 0:32], T.x1[:, 32:64], ADD),
+        lambda: tt(T.xi[:, :], T.x2[:, :], T.sh[:, :], MUL),
+        lambda: ts(T.xj[:, :], T.xi[:, :], 2047, AND),
+    ], [
+        lambda: tt(T.y1[:, :], half(T.g2, 2), half(T.g2, 3), ADD),
+        lambda: tt(T.st1[:, :], T.ee[:, 0:128:32], T.kc[:, :], SUB),
+        lambda: tt(half(T.z1, 0), half(T.ee, 0), half(T.ee, 1), ADD),
+        lambda: tt(T.st2[:, :], T.st1[:, :], T.tt[:, 0:4], ADD),
+        lambda: tt(half(T.z1, 1), half(T.ee, 2), half(T.ee, 3), ADD),
+        lambda: ts(T.y2[:, :], half(T.e3b, 1), 2.0, MUL),
+        lambda: tt(T.z[:, :], half(T.z1, 0), half(T.z1, 1), ADD),
+        lambda: tt(T.y4[:, :], T.y1[:, :], T.y2[:, :], ADD),
+        lambda: ts(T.sh[:, :], T.z[:, :], -1.0 / 2048, MUL, 1.0 + 1.0 / 2048, ADD),
+        lambda: ts(T.y3[:, :], T.z[:, :], 2.0, GE, 0.5, MUL),
+        None,
+        lambda: tt(T.y5[:, :], T.y3[:, :], T.y4[:, :], ADD),
+    ])
+    vw(v)
     for k in range(4):
         a = 16 * (k // 2)
-        v = tt(T.dd[:, 16 * k:16 * k + 16], T.x2[:, a:a + 16], T.x2[:, 32 + a:48 + a], ADD)
+        v = vec(V.tensor_copy(T.dd[:, 16 * k:16 * k + 16], T.xj[:, a:a + 16]))
     vw(v)
-    vw(vec(V.transpose(T.td[:, :], T.dd[:, :])))
+    v = vec(V.transpose(T.td[:, :], T.dd[:, :]))
+    v_win = ts(T.win[:, :], T.y5[:, :], 2.0, MUL)
+    vw(v)
     vec(V.tensor_copy(T.off[:, 0:64:2], T.td[:, 0:32]))
     v_off = vec(V.tensor_copy(T.off[:, 1:64:2], T.td[:, 32:64]))
 
@@ -295,53 +351,52 @@ def rank_program(g, core, T, topo):
 
     Y.wait_ge(S.v, v_off)
     turn(1, S.l1)
-    vw(tt(T.wv[:, :], T.ee[:, :], T.wt[:, :], MUL))
-    vw(tt(T.y1[:, :], T.wv[:, 0:128], T.wv[:, 128:256], ADD))
-    vw(tt(T.y2[:, :], T.y1[:, 0:64], T.y1[:, 64:128], ADD))
-    v_win = tt(T.win[:, :], T.y2[:, 0:32], T.y2[:, 32:64], ADD)
 
     P.wait_ge(S.aap, n_near)
     P.wait_ge(S.aa, n_near)
-    pair(96 - 64 * kind, 32 - 32 * kind, 96 - 96 * kind)
-    Y.wait_ge(S.ac, n_far + n_near)
+    pair(96 - 64 * pos, 32 - 32 * pos, 96 - 96 * pos, range(8))
+    Y.wait_ge(S.ac, n_ac)
     turn(2, S.l2)
     turn(3, S.l2)
     Y.wait_ge(S.v, v_win)
     Y.dma_start(T.wn[:, :], T.win[:, :]).then_inc(S.st, 16)
     pick_of = lambda q, a, b: T.p[:, 768 * q:768 * q + 768].indirect(T.off[:, 32 * q + a // 16:32 * q + b // 16])
-    P.wait_ge(S.ab, n_far * len(same))
+    for c in direct:
+        P.wait_ge(codes_of(c), n_far)
     P.wait_ge(S.abp, n_far * len(same))
-    P.wait_ge(S.ac, n_far + n_near)
-    ready = []
+    EARLY = 1
+    ready = [three(q, direct, True, True) for q in range(EARLY)]
+    P.wait_ge(S.ac, n_ac)
     for q in range(8):
-        for k in range(2):
-            done = product(q, (2 * q + k) % 8, T.cb[:, 288 * k:288 * k + 288], T.pb[:, 288 * k:288 * k + 288], 288, 0, 288, 192 + 288 * k)
-        ready.append(done)
+        if q < EARLY:
+            ready[q] += three(q, arrive[1::2], False, q == 0)
+        else:
+            ready.append([product(q, T.cb, (T.pb, 0), 32 + 288 * k, 288, 0, 288, 192 + 288 * k) for k in range(2)])
         if q == 1:
             A.wait_ge(S.v, v_off)
-            A.wait_ge(S.s, ready[0])
+            for sem, k in ready[0]:
+                A.wait_ge(sem, k)
             s_half = inc("s", A.activation(T.ya[:, 256:512], pick_of(0, 256, 512), COPY))
-
-    vw(v_off)
 
     def pick(q, a, b, last):
         out = T.ya[:, a:b]
-        V.wait_ge(S.s, ready[q])
+        for sem, k in ready[q]:
+            V.wait_ge(sem, k)
         if last:
             vw(last)
         return vec(V.tensor_tensor(out, pick_of(q, a, b), out, ADD) if last else V.tensor_copy(out, pick_of(q, a, b)))
 
-    last = pick(1, 0, 256, pick(0, 0, 256, 0))
-    V.wait_ge(S.s, s_half)
-    last = pick(1, 256, 512, last)
-    for q in range(2, 6):
+    last = [pick(0, 0, 256, 0), n["v"]]
+    for q in range(1, 8):
         if q in (2, 4):
             V.wait_ge(*((S.l1, 32) if q == 2 else (S.l2, 64)))
-        last = pick(q, 0, 512, last)
-    for a in (0, 256):
-        k = pick(7, a, a + 256, pick(6, a, a + 256, last))
-        Y.wait_ge(S.v, k)
-        Y.dma_start(T.y[:, a:a + 256], T.ya[:, a:a + 256]).then_inc(S.st, 16)
+        for k in range(2):
+            if (q, k) == (1, 1):
+                V.wait_ge(S.s, s_half)
+            last[k] = pick(q, 256 * k, 256 * k + 256, last[k])
+    for k in range(2):
+        Y.wait_ge(S.v, last[k])
+        Y.dma_start(T.y[:, 256 * k:256 * k + 256], T.ya[:, 256 * k:256 * k + 256]).then_inc(S.st, 16)
     Y.wait_ge(S.st, 48)
     g.wait_ge(S.loc, n["loc"])
     g.wait_ge(S.v, n["v"])

@@ -4,24 +4,24 @@ from concourse.mybir import dt, AluOpType, ActivationFunctionType
 F4, F, B = "float8_e4m3fn_x4", "float32", "bfloat16"
 SCRATCH = {}
 for _names, _w, _t in (
-        ("uw", 64, B), ("xs", 2048, B), ("zt", 560, B), ("wz", 4096, B), ("h", 512, B),
+        ("uw", 32, B), ("uq", 16, B), ("xs", 2048, B), ("zt", 560, B), ("wz", 4096, B), ("h", 512, B),
         ("cz", 140, F4), ("pz", 140, "uint8"), ("cx", 256, F4), ("cw", 1024, F4), ("pw", 1024, "uint8"),
         ("ca", 256, F4), ("pa", 992, "uint8"), ("cb", 640, F4), ("pb", 640, "uint8"),
-        ("ia ib", 8, "int32"), ("fa g8", 8, F), ("kc st1 st2 h4", 4, F),
-        ("v32 ms sm m1 b0 b1 g2 r128 ee cs4 u uv", 128, F), ("xi xj", 32, "int32"),
-        ("oz", 36, "uint16"), ("ic c1 r16 one", 32, F), ("cj ya", 512, F), ("hm ls", 96, F), ("acc cc", 224, F),
-        ("r", 256, F), ("s2 m2 e3b b2 x1 z1 dd td", 64, F), ("l", 528, F),
-        ("cs t1 t2 t3 v1 v3 tt tu tv tw x2 z sh y1 y2 y3 y4 y5 win", 32, F),
+        ("ia ib", 8, "int32"), ("fa", 8, F), ("kc st1 st2", 4, F),
+        ("v32 ms sm m1 b0 b1 bi g2 gs r128 ee cs4 u uv", 128, F), ("xi xj", 32, "int32"),
+        ("oz", 4, "uint16"), ("ic", 33, F), ("c1 r16 one", 32, F), ("cj ya", 512, F), ("k4 hm ls", 96, F), ("acc cc", 224, F),
+        ("r", 256, F), ("s2 m2 e3b b2 x1 dd td", 64, F), ("l tb", 528, F),
+        ("oc", 2, "uint16"), ("od", 4, "uint16"), ("t1", 16, F), ("t2", 4, F), ("cs v1 v3 tt tu tv tw", 32, F), ("rk", 768, F), ("win", 1024, F),
         ("ow", 32, "uint16"), ("og", 24, "uint16"), ("off", 256, "uint16"), ("p", 6144, F)):
     for _k in _names.split():
         SCRATCH[_k] = ("sbuf", [128, _w], _t)
 SCRATCH["ps"] = ("psum", [128, 4096], F)
 SEMAPHORES = ["lu", "lx0", "lx1", "lx2", "lw0", "lw1", "lw2", "lw3", "gi", "v", "s", "pe", "l1", "l2", "st",
-              "aa", "aap", "abp", "ac", "loc"] + ["%s%d" % (_k, _s) for _k in "ab" for _s in range(8)]
+              "aa", "aap", "ac0", "ac1", "ac2", "loc"] + ["%s%d" % (_k, _s) for _k in "abc" for _s in range(8)]
 
 ADD, SUB, MUL, MAX, MIN = AluOpType.add, AluOpType.subtract, AluOpType.mult, AluOpType.max, AluOpType.min
 GE, GT, EQ, NE, AND = AluOpType.is_ge, AluOpType.is_gt, AluOpType.is_equal, AluOpType.not_equal, AluOpType.bitwise_and
-COPY = ActivationFunctionType.Copy
+COPY, SAME, RELU = ActivationFunctionType.Copy, ActivationFunctionType.Identity, ActivationFunctionType.Relu
 
 
 def bitrev(s):
@@ -91,21 +91,21 @@ def rank_program(g, core, T, topo):
         g.remote_dma_fused([RemoteDMATransfer(dst_ids=[did(c) for c, _ in to], dma_engine_mask=sum(1 << e for e in m), remote_sem=sem,
                                               srcs=[src], dsts=[d for _, d in to], alu_op=0) for m, sem, src, to in transfers], local_sem=S.loc)
 
-    Y.dma_start(T.uw[:, 0:64], T.us[:, 0:64]).then_inc(S.lu, 16)
-    for k, (q, a, b) in enumerate(((A, 0, 1024), (Y, 1024, 1536), (A, 1536, 2048))):
+    Y.dma_start(T.uw[:, :], T.us[:, 0:32]).then_inc(S.lu, 16)
+    for k, (q, a, b) in enumerate(((A, 0, 1024), (Y, 1024, 1536), (Y, 1536, 2048))):
         q.dma_start(T.xs[:, a:b], T.x[:, a:b]).then_inc(S["lx%d" % k], 16)
 
     k_p = inc("gi", g.iota(T.ia[:, 0:1], [[0, 1]], 0, 1))
-    k_a = iota(T.g8[:, :], [[4, 8]], 0, 0)
     k_b = iota(T.v32[:, :], [[1, 4], [0, 32]], 0, 0)
-    iota(T.ic[:, :], [[-1, 32]], 512, 0)
+    iota(T.ic[:, :], [[-1, 33]], 512, 0)
+    iota(T.k4[:, :], [[0, 24], [1, 4]], 0, 0)
     k_c = iota(T.cj[:, :], [[4, 32], [128, 16]], 0, 0)
 
-    def load_w(k):
-        for t in (2 * k, 2 * k + 1):
+    def load_w(k, q=Y, tiles=(0, 1)):
+        for t in (2 * k + i for i in tiles):
             for a in range(4):
                 r = 16 * ((2 * a + t) % 8)
-                Y.dma_start(T.wz[r:r + 16, 512 * t + 128 * a:512 * t + 128 * a + 128], T.w[r:r + 16, 128 * a:128 * a + 128]).then_inc(S["lw%d" % k], 16)
+                q.dma_start(T.wz[r:r + 16, 512 * t + 128 * a:512 * t + 128 * a + 128], T.w[r:r + 16, 128 * a:128 * a + 128]).then_inc(S["lw%d" % k], 16)
 
     def zeros(k):
         Y.wait_ge(S.v, vec(V.memset(T.wz[:, 1024 * k:1024 * k + 1024], 0.0)))
@@ -114,40 +114,42 @@ def rank_program(g, core, T, topo):
         V.wait_ge(S["lw%d" % k], 128)
         return vec(V.quantize_mx(T.cw[:, 256 * k:256 * k + 256], T.pw[:, 256 * k:256 * k + 256], T.wz[:, 1024 * k:1024 * k + 1024]))
 
-    vec(V.memset(T.oz[:, :], 32))
     zeros(3)
     A.wait_ge(S.v, n["v"])
-    Y.wait_ge(S.s, inc("s", A.activation(T.wz[:, 0:1024], T.wz[:, 3072:4096], COPY)))
-    V.wait_ge(S.gi, k_a)
-    ts(T.ib[:, 0:1], T.ia[:, 0:1], 3, AND)
-    ts(T.ib[:, 1:2], T.ia[:, 0:1], 15, AND)
-    vw(ts(T.ib[:, 2:3], T.ia[:, 0:1], 12, AND, 2, AluOpType.arith_shift_right))
-    vw(vec(V.tensor_copy(T.fa[:, 0:3], T.ib[:, 0:3])))
-    v_oz = ts(T.oz[:, 3:32:4], T.g8[:, :], T.fa[:, 0:1], ADD)
-    ts(T.fa[:, 4:5], T.fa[:, 1:2], 32.0, MUL)
-    load_w(0)
+    s_z = [inc("s", A.activation(T.wz[:, 1024 * k:1024 * k + 1024], T.wz[:, 3072:4096], COPY)) for k in (0, 2)]
     zeros(1)
     load_w(1)
-    V.wait_ge(S.gi, k_b)
-    ts(T.ms[:, :], T.v32[:, :], T.fa[:, 0:1], EQ)
-    zeros(2)
-    load_w(2)
-    load_w(3)
+    Y.wait_ge(S.s, s_z[0])
+    load_w(0)
+    Y.wait_ge(S.s, s_z[1])
+    load_w(2, Y, (0,))
+    A.wait_ge(S.s, s_z[1])
+    load_w(3, A)
+    load_w(2, A, (1,))
 
-    A.wait_ge(S.lu, 16)
-    A.wait_ge(S.v, v_oz)
-    s_zt = inc("s", A.activation(T.zt[:, 0:320], T.uw[:, 0:64].indirect(T.oz[:, 0:20]), COPY))
+    V.wait_ge(S.gi, k_p)
+    ts(T.ib[:, 0:1], T.ia[:, 0:1], 3, AND)
+    ts(T.ib[:, 1:2], T.ia[:, 0:1], 15, AND)
+    ts(T.ib[:, 2:3], T.ia[:, 0:1], 12, AND, 2, AluOpType.arith_shift_right)
+    vw(ts(T.ib[:, 3:4], T.ia[:, 0:1], 4, AluOpType.arith_shift_right))
+    v = vec(V.tensor_copy(T.fa[:, 0:4], T.ib[:, 0:4]))
+    vec(V.memset(T.zt[:, :], 0.0))
+    vw(v)
+    ts(T.oz[:, 0:1], T.fa[:, 3:4], 4.0, MUL, T.fa[:, 0:1], ADD)
+    vw(ts(T.oz[:, 2:3], T.fa[:, 3:4], 64.0, MUL, T.fa[:, 1:2], ADD))
+
     V.wait_ge(S.lu, 16)
-    vw(v_oz)
-    v_zt = vec(V.tensor_copy(T.zt[:, 320:560], T.uw[:, 0:64].indirect(T.oz[:, 20:35])))
+    v_uq = vec(V.tensor_copy(T.uq[:, :], T.uw[:, 0:32].indirect(T.oz[:, 0:1])))
 
     px = 224 + 512 * pos
     quarter = [(T.cb[:, 0:128], T.pb[:, 0:128]), (T.cb[:, 512:640], T.pb[:, 512:640]),
                (T.cx[:, 0:128], T.pa[:, px:px + 128]), (T.cx[:, 128:256], T.pa[:, px + 128:px + 256])]
     v_x = []
     for q in range(4):
+        if q == 1:
+            vw(v_uq)
+            v_zt = vec(V.tensor_copy(T.zt[:, 48:560].indirect(T.oz[:, 2:3]), T.uq[:, :]))
         if q == 2:
-            V.wait_ge(S.s, s_zt)
             vw(v_zt)
             v_cz = vec(V.quantize_mx(T.cz[:, :], T.pz[:, :], T.zt[:, :]))
         if q != 1:
@@ -158,6 +160,8 @@ def rank_program(g, core, T, topo):
         P.wait_ge(S.v, max(v_x[q], v_cz))
         k_sc = inc("pe", P.matmul_mx(T.ps[:, 3584:3712], T.cz[:, a:a + 128], T.pz[:, a:a + 128], *quarter[q], q == 0, q == 3))
 
+    V.wait_ge(S.gi, k_b)
+    vw(ts(T.ms[:, :], T.v32[:, :], T.fa[:, 0:1], EQ))
     V.wait_ge(S.pe, k_sc)
     me = bitrev(rank)
     R = lambda b, q=1: T.r[:, 32 * b:32 * (b + q)]
@@ -168,80 +172,116 @@ def rank_program(g, core, T, topo):
     sem_of = lambda c: S["a%d" % cores.index(c)]
     send((eng_far, sem_of(core), own, [(c, own) for c in far]))
     send((eng_near, sem_of(core), own, [(mate, own)]))
+    A.wait_ge(S.gi, k_c)
+    s_tb = inc("s", A.activation(T.tb[:, 0:33], T.ic[:, :], SAME, bias=512.0, scale=-1.0))
+    for j in (1, 2, 4, 8):
+        A.wait_ge(S.s, s_tb)
+        s_tb = inc("s", A.activation(T.tb[:, 33 * j:66 * j], T.tb[:, 0:33 * j], SAME, bias=-64.0 * j))
+    for s in range(8):
+        inc("s", A.activation(T.rk[:, start_of(s):start_of(s) + 96], T.k4[:, :], SAME, bias=float(s), scale=0.0))
 
     h0 = 128 * (1 - pos)
     vec(V.memset(T.h[:, 384 * pos:384 * pos + 128], 0.0))
     V.wait_ge(S.gi, k_c)
-    ts(T.c1[:, :], T.ic[:, :], T.fa[:, 4:5], SUB)
-    ts(T.h4[:, :], T.v32[:, 0:128:32], T.fa[:, 2:3], NE, 4096.0, MUL)
-    for t in (T.one, T.r16, T.r128):
+    vw(ts(T.fa[:, 4:5], T.fa[:, 1:2], 32.0, MUL))
+    ts(T.c1[:, :], T.ic[:, 0:32], T.fa[:, 4:5], SUB)
+    ts(T.fa[:, 5:6], T.fa[:, 1:2], 33.0, MUL)
+    ts(T.fa[:, 6:7], T.fa[:, 1:2], 64.0, MUL, -64.0, ADD)
+    ts(T.fa[:, 7:8], T.fa[:, 1:2], -1.0, ADD, T.fa[:, 4:5], MUL)
+    ts(T.hm[:, :], T.k4[:, :], T.fa[:, 2:3], NE, 4096.0, MUL)
+    for t in (T.r16, T.r128, T.one):
         v = vec(V.memset(t[:, :], 1.0))
-    vw(v)
-    for k in range(4):
-        ts(T.hm[:, k:96:4], T.one[:, 0:24], T.h4[:, k:k + 1], MUL)
-    vec(V.memset(T.r16[:, 0:32:16], 0.0))
-    vec(V.memset(T.r128[:, 0:128:32], 0.0))
     vec(V.memset(T.tt[:, :], 0.0))
+    for k in range(4):
+        ts(T.od[:, k:k + 1], T.fa[:, 1:2], 16.0 * (k // 2), ADD)
     for b in range(4):
         vec(V.memset(T.kc[:, b:b + 1], float(start_of(bitrev(b)) + 96 + 2048 * (start_of(bitrev(b + 4)) + 96))))
-    pack(0)
-    pack(1)
+    vw(v)
+    vec(V.memset(T.r16[:, 0:32:16], 0.0))
+    vec(V.memset(T.r128[:, 0:128:32], 0.0))
+    for k in (1, 0, 3):
+        pack(k)
 
     half = lambda t, k: t[:, 32 * k:32 * k + 32]
     blk = lambda c: bitrev(cores.index(c))
     beats = lambda k, c, other: tt(half(T.cc, k), own, other, GT if cores.index(c) < rank else GE)
     m1 = lambda j: tt(half(T.m1, j), R(j), R(j + 4), MAX)
     b0 = lambda j: tt(half(T.b0, j), R(j + 4), R(j), GT)
-    b1 = lambda j: ts(half(T.b1, j), half(T.b0, j), 2047.0, MUL, 1.0, ADD)
     m2 = lambda j: tt(half(T.m2, j), half(T.m1, j), half(T.m1, j + 2), MAX)
     b2 = lambda j: tt(half(T.b2, j), half(T.m1, j + 2), half(T.m1, j), GT)
     j0, jx, jy, jz = me & 3, blk(arrive[1]) & 3, blk(arrive[3]) & 3, blk(arrive[5]) & 3
-    beside = [[], [(m1, jx), (b0, jx)], [(b1, jx)], [(m1, j0), (b0, j0)], [(b1, j0), (m1, jy)], [(b0, jy)], [(m1, jz)]]
+    order = arrive[:5] + [mate] + arrive[5:]
+    won = lambda k: half(T.acc if k else T.cc, k)
+    both = lambda k: tt(won(k), won(k - 1), half(T.cc, k), MUL)
+
+    def compare(k):
+        V.wait_ge(sem_of(order[k]), n_near if order[k] == mate else n_far)
+        return beats(k, order[k], R(blk(order[k])))
+
     vw(n["v"])
-    for k, c in enumerate(arrive[:3] + [mate] + arrive[3:]):
-        V.wait_ge(sem_of(c), n_near if c == mate else n_far)
-        v = beats(k, c, R(blk(c)))
-        vw(v - 1)
-        for call, j in beside[k]:
-            call(j)
-        if k:
-            vw(v)
-            v_e = tt(half(T.acc, k), so_far, half(T.cc, k), MUL)
-        else:
-            pack(2)
-        so_far = half(T.acc if k else T.cc, k)
-    e = so_far
-    m2(1 - (jz & 1))
+    compare(0)
+    pack(2)
+    for k in (1, 2):
+        v = compare(k)
+        (m1, b0)[k - 1](jx)
+        vw(v)
+        both(k)
+    v = compare(3)
+    for k in (4, 5):
+        compare(k)
+        vw(v)
+        v = both(k - 1)
+    m1(jy)
+    vw(v)
+    both(5)
+    v = compare(6)
+    m1(jz)
+    vw(v)
+    v_e = both(6)
+    e = won(6)
+    m1(j0)
+    b0(j0)
     vw(v_e)
     v_cs = scan(T.cs[:, :], T.one[:, :], e, ADD, SUB)
     tt(T.v1[:, :], e, T.c1[:, :], MUL)
+    b0(jz)
     vw(v_cs)
-    v_t1 = vec(V.transpose(T.t1[:, :], T.cs[:, :]))
-    vw(v_t1 - 1)
+    A.wait_ge(S.v, ts(T.oc[:, 0:1], T.cs[:, 31:32], T.fa[:, 5:6], ADD))
+    A.wait_ge(S.s, s_tb)
+    s_pre = inc("s", A.activation(T.t1[:, :], T.tb[:, 0:528].indirect(T.oc[:, 0:1]), RELU, bias=T.fa[:, 6:7], accum_out=T.t2[:, 0:1]))
+    v = m2(jz & 1)
+    vw(v_cs + 1)
     tt(T.v3[:, :], T.v1[:, :], T.cs[:, :], ADD)
-    vw(v_t1)
-    v_t2 = scan(T.t2[:, :], T.r16[:, :], T.t1[:, :])
-    m2(jz & 1)
-    vw(v_t2)
-    v_t3 = vec(V.transpose(T.t3[:, :], T.t2[:, :]))
+    m2(1 - (jz & 1))
     b2(jz & 1)
-    vw(v_t3)
-    v_ow = ts(T.ow[:, :], T.v3[:, :], T.t3[:, 31:32], ADD, T.cs[:, 31:32], SUB)
+    A.wait_ge(S.v, b0(jy))
+    inc("s", A.activation(T.b1[:, :], T.b0[:, :], SAME, bias=1.0, scale=2047.0))
+    inc("s", A.activation(T.bi[:, :], T.b0[:, :], SAME, bias=1.0, scale=1.0 / 2048 - 1.0))
+    vw(v + 2)
+    V.wait_ge(S.s, s_pre)
+    v_ow = ts(T.ow[:, :], T.v3[:, :], T.t2[:, 0:1], ADD, T.fa[:, 7:8], SUB)
     tt(half(T.e3b, 0), half(T.m2, 0), half(T.m2, 1), GE)
+    tt(half(T.e3b, 1), half(T.m2, 1), half(T.m2, 0), GT)
     vw(v_ow)
     v_l = vec(V.tensor_copy(T.l[:, 0:528].indirect(T.ow[:, 0:32]), T.cj[:, :]))
-    tt(half(T.e3b, 1), half(T.m2, 1), half(T.m2, 0), GT)
+    z = jz & 1
+    upper = lambda k: tt(half(T.g2, 2 + k), half(T.e3b, k), half(T.b2, k), MUL)
+    lower = lambda k: tt(half(T.g2, k), half(T.e3b, k), half(T.g2, 2 + k), SUB)
+    vw(v_l - 1)
+    b2(1 - z)
+    upper(z)
     vw(v_l)
     v_ls = scan(T.ls[:, :], T.hm[:, :], T.l[:, 417:513], MIN, MAX)
-    b2(1 - (jz & 1))
+    vw(v_ls - 1)
+    upper(1 - z)
     vw(v_ls)
     v_og = ts(T.og[:, :], T.ls[:, 3:96:4], T.fa[:, 0:1], ADD)
     A.wait_ge(S.v, v_og)
     s_h = inc("s", A.activation(T.h[:, h0 + 192:h0 + 384], T.xs[:, 0:2048].indirect(T.og[:, 12:24]), COPY))
-    b0(jz)
+    lower(z)
     vw(v_og)
     v_h = vec(V.tensor_copy(T.h[:, h0:h0 + 192], T.xs[:, 0:2048].indirect(T.og[:, 0:12])))
-    tt(half(T.g2, 2), half(T.e3b, 0), half(T.b2, 0), MUL)
+    lower(1 - z)
     vw(v_h)
     V.wait_ge(S.s, s_h)
     c0, cq = 32 + 96 * pos, 128 * pos
@@ -251,16 +291,14 @@ def rank_program(g, core, T, topo):
     wide = T.pa[:, 224 + 384 * pos:608 + 384 * pos]
     codes_of = lambda c: S["b%d" % cores.index(c)]
     send((eng_far, codes_of(core), by(T.ca, c0), [(c, by(T.cb, col(core, c))) for c in same]), (eng_near, S.aap, wide, [(mate, wide)]))
+    send((eng_near, S.aa, by(T.ca, c0), [(mate, by(T.ca, c0))]))
     g.wait_ge(S.aap, n_near)
-    send((eng_far, S.abp, T.pa[:, 512:704], [(c, T.pb[:, slot(core, c):slot(core, c) + 192]) for c in same]),
-         *[(m, S.aa, by(T.ca, c0 + a, 48), [(mate, by(T.ca, c0 + a, 48))]) for m, a in ((near_a, 0), (near_b, 48))])
+    planes_of = lambda c: S["c%d" % cores.index(c)]
+    send((eng_far, planes_of(core), T.pa[:, 512:704], [(c, T.pb[:, slot(core, c):slot(core, c) + 192]) for c in same]))
     direct = arrive[::2]
-    n_ac = 0
-    for step in (((direct[0], eng_near),), ((direct[1], eng_near), (direct[2], eng_far))):
-        for c, m in step:
-            g.wait_ge(codes_of(c), n_far)
-            n_ac += len(m)
-        send(*[(m, S.ac, by(T.cb, col(c)), [(mate, by(T.cb, col(c)))]) for c, m in step])
+    for k, c in enumerate(direct):
+        g.wait_ge(codes_of(c), n_far)
+        send((eng_near, S["ac%d" % k], by(T.cb, col(c)), [(mate, by(T.cb, col(c)))]))
 
     freed = [None] * 8
     bank = [0]
@@ -278,22 +316,18 @@ def rank_program(g, core, T, topo):
         freed[b] = (S.v, vec(V.tensor_copy(out, res))) if by_vector else (S.s, inc("s", A.activation(out, res, COPY)))
         return freed[b]
 
-    def pair(a, skip, at, tiles, by_vector=False):
-        for q in tiles:
-            product(q, T.ca, (T.pa, 480), a, 128, skip, 96, at, by_vector)
+    def near(a, skip, at):
+        for q in range(8):
+            product(q, T.ca, (T.pa, 480), a, 128, skip, 96, at)
 
-    def three(q, blocks, two_by_vector, one_by_vector):
-        a, b, c = sorted(col(x) for x in blocks)
-        two, one = (a, c) if b == a + 96 else (b, a)
-        skip = 32 if one == 32 else 0
-        return [product(q, T.cb, (T.pb, 0), two, 192, 0, 192, 160 + two, two_by_vector),
-                product(q, T.cb, (T.pb, 0), one - skip, 128, skip, 96, 160 + one, one_by_vector)]
-
-    P.wait_ge(S.v, pack(3))
-    pair(cq, c0 - cq, 96 * pos, range(8))
+    P.wait_ge(S.v, v_q)
+    near(cq, c0 - cq, 96 * pos)
+    P.wait_ge(S.aap, n_near)
+    P.wait_ge(S.aa, n_near)
+    near(96 - 64 * pos, 32 - 32 * pos, 96 - 96 * pos)
 
     def chain(links, beside):
-        v = n["v"]
+        v = v_q - 1
         for k, link in enumerate(links):
             vw(v)
             v = link()
@@ -301,11 +335,6 @@ def rank_program(g, core, T, topo):
                 beside[k]()
         return v
 
-    v = tt(half(T.g2, 3), half(T.e3b, 1), half(T.b2, 1), MUL)
-    b1(jy)
-    b1(jz)
-    vw(v)
-    tt(T.g2[:, 0:64], T.e3b[:, :], T.g2[:, 64:128], SUB)
     v = chain([
         lambda: tt(T.ee[:, :], T.g2[:, :], T.b1[:, :], MUL),
         lambda: scan(T.cs4[:, :], T.r128[:, :], T.ee[:, :], MUL, SUB),
@@ -315,33 +344,20 @@ def rank_program(g, core, T, topo):
         lambda: vec(V.transpose(T.tw[:, :], T.tv[:, :])),
         lambda: tt(T.ee[:, 0:128:32], T.st2[:, :], T.tw[:, 0:4], SUB),
         lambda: scan(T.u[:, :], T.r128[:, :], T.ee[:, :], MUL, SUB),
-        lambda: tt(T.uv[:, :], T.u[:, :], T.g2[:, :], MUL),
+        lambda: tt(T.uv[:, :], T.u[:, :], T.gs[:, :], MUL),
         lambda: tt(T.x1[:, :], T.uv[:, 0:64], T.uv[:, 64:128], ADD),
-        lambda: tt(T.x2[:, :], T.x1[:, 0:32], T.x1[:, 32:64], ADD),
-        lambda: tt(T.xi[:, :], T.x2[:, :], T.sh[:, :], MUL),
+        lambda: tt(T.xi[:, :], T.x1[:, 0:32], T.x1[:, 32:64], ADD),
         lambda: ts(T.xj[:, :], T.xi[:, :], 2047, AND),
     ], [
-        lambda: tt(T.y1[:, :], half(T.g2, 2), half(T.g2, 3), ADD),
-        lambda: tt(T.st1[:, :], T.ee[:, 0:128:32], T.kc[:, :], SUB),
-        lambda: tt(half(T.z1, 0), half(T.ee, 0), half(T.ee, 1), ADD),
-        lambda: tt(T.st2[:, :], T.st1[:, :], T.tt[:, 0:4], ADD),
-        lambda: tt(half(T.z1, 1), half(T.ee, 2), half(T.ee, 3), ADD),
-        lambda: ts(T.y2[:, :], half(T.e3b, 1), 2.0, MUL),
-        lambda: tt(T.z[:, :], half(T.z1, 0), half(T.z1, 1), ADD),
-        lambda: tt(T.y4[:, :], T.y1[:, :], T.y2[:, :], ADD),
-        lambda: ts(T.sh[:, :], T.z[:, :], -1.0 / 2048, MUL, 1.0 + 1.0 / 2048, ADD),
-        lambda: ts(T.y3[:, :], T.z[:, :], 2.0, GE, 0.5, MUL),
         None,
-        lambda: tt(T.y5[:, :], T.y3[:, :], T.y4[:, :], ADD),
+        lambda: tt(T.st1[:, :], T.ee[:, 0:128:32], T.kc[:, :], SUB),
+        lambda: tt(T.gs[:, 0:64], T.g2[:, 0:64], T.bi[:, 0:64], MUL),
+        lambda: tt(T.st2[:, :], T.st1[:, :], T.tt[:, 0:4], ADD),
+        lambda: tt(T.gs[:, 64:128], T.g2[:, 64:128], T.bi[:, 64:128], MUL),
     ])
     vw(v)
-    for k in range(4):
-        a = 16 * (k // 2)
-        v = vec(V.tensor_copy(T.dd[:, 16 * k:16 * k + 16], T.xj[:, a:a + 16]))
-    vw(v)
-    v = vec(V.transpose(T.td[:, :], T.dd[:, :]))
-    v_win = ts(T.win[:, :], T.y5[:, :], 2.0, MUL)
-    vw(v)
+    vw(vec(V.tensor_copy(T.dd[:, :], T.xj[:, 0:32].indirect(T.od[:, 0:4]))))
+    vw(vec(V.transpose(T.td[:, :], T.dd[:, :])))
     vec(V.tensor_copy(T.off[:, 0:64:2], T.td[:, 0:32]))
     v_off = vec(V.tensor_copy(T.off[:, 1:64:2], T.td[:, 32:64]))
 
@@ -352,31 +368,38 @@ def rank_program(g, core, T, topo):
     Y.wait_ge(S.v, v_off)
     turn(1, S.l1)
 
-    P.wait_ge(S.aap, n_near)
-    P.wait_ge(S.aa, n_near)
-    pair(96 - 64 * pos, 32 - 32 * pos, 96 - 96 * pos, range(8))
-    Y.wait_ge(S.ac, n_ac)
+    Y.wait_ge(planes_of(direct[2]), n_far)
     turn(2, S.l2)
     turn(3, S.l2)
-    Y.wait_ge(S.v, v_win)
-    Y.dma_start(T.wn[:, :], T.win[:, :]).then_inc(S.st, 16)
     pick_of = lambda q, a, b: T.p[:, 768 * q:768 * q + 768].indirect(T.off[:, 32 * q + a // 16:32 * q + b // 16])
-    for c in direct:
+    ready = [[], [], []]
+    chip = lambda q, c, by_vector: ready[q].append(product(q, T.cb, (T.pb, 0), slot(c, core), 192, 0, 192, 160 + slot(c, core), by_vector))
+    for k, c in enumerate(direct):
         P.wait_ge(codes_of(c), n_far)
-    P.wait_ge(S.abp, n_far * len(same))
-    EARLY = 1
-    ready = [three(q, direct, True, True) for q in range(EARLY)]
-    P.wait_ge(S.ac, n_ac)
-    for q in range(8):
-        if q < EARLY:
-            ready[q] += three(q, arrive[1::2], False, q == 0)
+        P.wait_ge(S["ac%d" % k], n_near)
+        P.wait_ge(planes_of(c), n_far)
+        if k < 2:
+            for q in range(3 - k):
+                chip(q, c, q == 2 - k)
         else:
+            for j in range(2):
+                a = slot(c, core) + 64 * j
+                ready[0].append(product(0, T.cb, (T.pb, 0), a, 128, 32 * j, 96, 160 + a + 32 * j, j == 1))
+            chip(1, c, False)
+    for q in range(8):
+        if q == 2:
+            chip(q, direct[1], False)
+            chip(q, direct[2], False)
+        elif q > 2:
             ready.append([product(q, T.cb, (T.pb, 0), 32 + 288 * k, 288, 0, 288, 192 + 288 * k) for k in range(2)])
         if q == 1:
             A.wait_ge(S.v, v_off)
             for sem, k in ready[0]:
                 A.wait_ge(sem, k)
             s_half = inc("s", A.activation(T.ya[:, 256:512], pick_of(0, 256, 512), COPY))
+
+    A.wait_ge(S.s, inc("s", A.activation(T.win[:, :], T.rk[:, 0:768].indirect(T.off[:, 0:64]), COPY)))
+    A.dma_start(T.wn[:, :], T.win[0:128:32, :]).then_inc(S.st, 16)
 
     def pick(q, a, b, last):
         out = T.ya[:, a:b]
@@ -386,6 +409,7 @@ def rank_program(g, core, T, topo):
             vw(last)
         return vec(V.tensor_tensor(out, pick_of(q, a, b), out, ADD) if last else V.tensor_copy(out, pick_of(q, a, b)))
 
+    vw(v_off)
     last = [pick(0, 0, 256, 0), n["v"]]
     for q in range(1, 8):
         if q in (2, 4):

from concourse.bass import DstId, RemoteDMATransfer
from concourse.mybir import dt, AluOpType, ActivationFunctionType

F4, F, B = "float8_e4m3fn_x4", "float32", "bfloat16"
SCRATCH = {}
for _names, _w, _t in (
        ("uw", 32, B), ("uq", 16, B), ("xs", 2048, B), ("zt", 560, B), ("wz", 4096, B), ("h", 512, B),
        ("cz", 140, F4), ("pz", 140, "uint8"), ("cx", 256, F4), ("cw", 1024, F4), ("pw", 1024, "uint8"),
        ("ca", 256, F4), ("pa", 992, "uint8"), ("cb", 640, F4), ("pb", 640, "uint8"),
        ("ia ib", 8, "int32"), ("fa", 8, F), ("kc st1 st2", 4, F),
        ("v32 ms sm m1 b0 b1 bi g2 gs r128 ee cs4 u uv", 128, F), ("xi xj", 32, "int32"),
        ("oz", 4, "uint16"), ("ic", 33, F), ("c1 r16 one", 32, F), ("cj ya", 512, F), ("k4 hm ls", 96, F), ("acc cc", 224, F),
        ("r", 256, F), ("s2 m2 e3b b2 x1 dd td", 64, F), ("l tb", 528, F),
        ("oc", 2, "uint16"), ("od", 4, "uint16"), ("t1", 16, F), ("t2", 4, F), ("cs v1 v3 tt tu tv tw", 32, F), ("rk", 768, F), ("win", 1024, F),
        ("ow", 32, "uint16"), ("og", 24, "uint16"), ("off", 256, "uint16"), ("p", 6144, F)):
    for _k in _names.split():
        SCRATCH[_k] = ("sbuf", [128, _w], _t)
SCRATCH["ps"] = ("psum", [128, 4096], F)
SEMAPHORES = ["lu", "lx0", "lx1", "lx2", "lw0", "lw1", "lw2", "lw3", "gi", "v", "s", "pe", "l1", "l2", "st",
              "aa", "aap", "ac0", "ac1", "ac2", "loc"] + ["%s%d" % (_k, _s) for _k in "abc" for _s in range(8)]

ADD, SUB, MUL, MAX, MIN = AluOpType.add, AluOpType.subtract, AluOpType.mult, AluOpType.max, AluOpType.min
GE, GT, EQ, NE, AND = AluOpType.is_ge, AluOpType.is_gt, AluOpType.is_equal, AluOpType.not_equal, AluOpType.bitwise_and
COPY, SAME, RELU = ActivationFunctionType.Copy, ActivationFunctionType.Identity, ActivationFunctionType.Relu


def bitrev(s):
    return (s & 1) * 4 + (s & 2) + (s >> 2)


def rank_program(g, core, T, topo):
    rank = T.rank_of(core)
    if rank is None:
        return
    S = T.sem
    V, A, P, Y = g.vector, g.scalar, g.tensor, g.sync
    n = {"v": 0, "s": 0, "pe": 0, "gi": 0, "loc": 0}

    def inc(q, call):
        n[q] += 1
        call.then_inc(S[q], 1)
        return n[q]

    vw = lambda k: V.wait_ge(S.v, k)
    vec = lambda call: inc("v", call)
    tt = lambda out, a, b, op: vec(V.tensor_tensor(out, a, b, op))
    ts = lambda out, a, s1, op, s2=None, op2=None: vec(V.tensor_scalar(out, a, s1, s2, op, op2) if op2 else V.tensor_scalar(out, a, s1, None, op))
    scan = lambda out, a, b, o0=MUL, o1=ADD: vec(V.tensor_tensor_scan(out, a, b, 0.0, o0, o1))
    iota = lambda out, pat, base, cm: inc("gi", g.iota(out, pat, base, cm, allow_small_or_imprecise_dtypes=True))

    cores = list(T.cores)
    chips = []
    for c in cores:
        if topo.chip(c) not in chips:
            chips.append(topo.chip(c))
    on = lambda ch: [c for c in cores if topo.chip(c) == ch]
    mychip = topo.chip(core)
    kind_of = lambda c: on(topo.chip(c)).index(c)
    kind = kind_of(core)
    mate = on(mychip)[1 - kind]

    def chips_from(c):
        a = chips.index(topo.chip(c))
        return sorted([chips[(a + d) % len(chips)] for d in range(1, len(chips))], key=lambda ch: topo.same_plane(ch, topo.chip(c)))

    far_of = lambda c: [on(ch)[k] for ch in chips_from(c) for k in (kind_of(c), 1 - kind_of(c))]
    far = far_of(core)
    same = far[::2]
    arrive = sorted(far, key=lambda c: far_of(c).index(core))
    flip = lambda ch: chips.index(ch) // 2
    pos_of = lambda c: kind_of(c) ^ flip(topo.chip(c))
    pos = pos_of(core)

    def slot(frm, to):
        a, b, c = sorted([ch for ch in chips if ch != topo.chip(to)], key=lambda ch: flip(ch) == flip(topo.chip(to)))
        return 32 + 192 * [a, c, b].index(topo.chip(frm))

    col = lambda c, to=core: slot(c, to) + 96 * pos_of(c)
    eng_far = [e for e in topo.engines(core, mate) if all(e in topo.engines(core, c) for c in far)]
    eng_near = [e for e in topo.engines(core, mate) if e not in eng_far]
    n_far, n_near = len(eng_far), len(eng_near)
    near_a, near_b = eng_near[:n_near // 2], eng_near[n_near // 2:]
    did = lambda c: DstId(rid=topo.addr(c)[0], pnc=topo.addr(c)[1])

    def start_of(s):
        c = cores[s]
        return 96 * pos_of(c) if c in on(mychip) else 160 + col(c)

    def send(*transfers):
        n["loc"] += sum(len(m) for m, _, _, _ in transfers)
        g.remote_dma_fused([RemoteDMATransfer(dst_ids=[did(c) for c, _ in to], dma_engine_mask=sum(1 << e for e in m), remote_sem=sem,
                                              srcs=[src], dsts=[d for _, d in to], alu_op=0) for m, sem, src, to in transfers], local_sem=S.loc)

    Y.dma_start(T.uw[:, :], T.us[:, 0:32]).then_inc(S.lu, 16)
    for k, (q, a, b) in enumerate(((A, 0, 1024), (Y, 1024, 1536), (Y, 1536, 2048))):
        q.dma_start(T.xs[:, a:b], T.x[:, a:b]).then_inc(S["lx%d" % k], 16)

    k_p = inc("gi", g.iota(T.ia[:, 0:1], [[0, 1]], 0, 1))
    k_b = iota(T.v32[:, :], [[1, 4], [0, 32]], 0, 0)
    iota(T.ic[:, :], [[-1, 33]], 512, 0)
    iota(T.k4[:, :], [[0, 24], [1, 4]], 0, 0)
    k_c = iota(T.cj[:, :], [[4, 32], [128, 16]], 0, 0)

    def load_w(k, q=Y, tiles=(0, 1)):
        for t in (2 * k + i for i in tiles):
            for a in range(4):
                r = 16 * ((2 * a + t) % 8)
                q.dma_start(T.wz[r:r + 16, 512 * t + 128 * a:512 * t + 128 * a + 128], T.w[r:r + 16, 128 * a:128 * a + 128]).then_inc(S["lw%d" % k], 16)

    def zeros(k):
        Y.wait_ge(S.v, vec(V.memset(T.wz[:, 1024 * k:1024 * k + 1024], 0.0)))

    def pack(k):
        V.wait_ge(S["lw%d" % k], 128)
        return vec(V.quantize_mx(T.cw[:, 256 * k:256 * k + 256], T.pw[:, 256 * k:256 * k + 256], T.wz[:, 1024 * k:1024 * k + 1024]))

    zeros(3)
    A.wait_ge(S.v, n["v"])
    s_z = [inc("s", A.activation(T.wz[:, 1024 * k:1024 * k + 1024], T.wz[:, 3072:4096], COPY)) for k in (0, 2)]
    zeros(1)
    load_w(1)
    Y.wait_ge(S.s, s_z[0])
    load_w(0)
    Y.wait_ge(S.s, s_z[1])
    load_w(2, Y, (0,))
    A.wait_ge(S.s, s_z[1])
    load_w(3, A)
    load_w(2, A, (1,))

    V.wait_ge(S.gi, k_p)
    ts(T.ib[:, 0:1], T.ia[:, 0:1], 3, AND)
    ts(T.ib[:, 1:2], T.ia[:, 0:1], 15, AND)
    ts(T.ib[:, 2:3], T.ia[:, 0:1], 12, AND, 2, AluOpType.arith_shift_right)
    vw(ts(T.ib[:, 3:4], T.ia[:, 0:1], 4, AluOpType.arith_shift_right))
    v = vec(V.tensor_copy(T.fa[:, 0:4], T.ib[:, 0:4]))
    vec(V.memset(T.zt[:, :], 0.0))
    vw(v)
    ts(T.oz[:, 0:1], T.fa[:, 3:4], 4.0, MUL, T.fa[:, 0:1], ADD)
    vw(ts(T.oz[:, 2:3], T.fa[:, 3:4], 64.0, MUL, T.fa[:, 1:2], ADD))

    V.wait_ge(S.lu, 16)
    v_uq = vec(V.tensor_copy(T.uq[:, :], T.uw[:, 0:32].indirect(T.oz[:, 0:1])))

    px = 224 + 512 * pos
    quarter = [(T.cb[:, 0:128], T.pb[:, 0:128]), (T.cb[:, 512:640], T.pb[:, 512:640]),
               (T.cx[:, 0:128], T.pa[:, px:px + 128]), (T.cx[:, 128:256], T.pa[:, px + 128:px + 256])]
    v_x = []
    for q in range(4):
        if q == 1:
            vw(v_uq)
            v_zt = vec(V.tensor_copy(T.zt[:, 48:560].indirect(T.oz[:, 2:3]), T.uq[:, :]))
        if q == 2:
            vw(v_zt)
            v_cz = vec(V.quantize_mx(T.cz[:, :], T.pz[:, :], T.zt[:, :]))
        if q != 1:
            V.wait_ge(S["lx%d" % max(q - 1, 0)], 16)
        v_x.append(vec(V.quantize_mx(*quarter[q], T.xs[:, 512 * q:512 * q + 512])))
    for q in range(4):
        a = 12 - 4 * q
        P.wait_ge(S.v, max(v_x[q], v_cz))
        k_sc = inc("pe", P.matmul_mx(T.ps[:, 3584:3712], T.cz[:, a:a + 128], T.pz[:, a:a + 128], *quarter[q], q == 0, q == 3))

    V.wait_ge(S.gi, k_b)
    vw(ts(T.ms[:, :], T.v32[:, :], T.fa[:, 0:1], EQ))
    V.wait_ge(S.pe, k_sc)
    me = bitrev(rank)
    R = lambda b, q=1: T.r[:, 32 * b:32 * (b + q)]
    own = R(me)
    vw(tt(T.sm[:, :], T.ps[:, 3584:3712], T.ms[:, :], MUL))
    vw(tt(T.s2[:, :], T.sm[:, 0:64], T.sm[:, 64:128], ADD))
    g.wait_ge(S.v, tt(own, T.s2[:, 0:32], T.s2[:, 32:64], ADD))
    sem_of = lambda c: S["a%d" % cores.index(c)]
    send((eng_far, sem_of(core), own, [(c, own) for c in far]))
    send((eng_near, sem_of(core), own, [(mate, own)]))
    A.wait_ge(S.gi, k_c)
    s_tb = inc("s", A.activation(T.tb[:, 0:33], T.ic[:, :], SAME, bias=512.0, scale=-1.0))
    for j in (1, 2, 4, 8):
        A.wait_ge(S.s, s_tb)
        s_tb = inc("s", A.activation(T.tb[:, 33 * j:66 * j], T.tb[:, 0:33 * j], SAME, bias=-64.0 * j))
    for s in range(8):
        inc("s", A.activation(T.rk[:, start_of(s):start_of(s) + 96], T.k4[:, :], SAME, bias=float(s), scale=0.0))

    h0 = 128 * (1 - pos)
    vec(V.memset(T.h[:, 384 * pos:384 * pos + 128], 0.0))
    V.wait_ge(S.gi, k_c)
    vw(ts(T.fa[:, 4:5], T.fa[:, 1:2], 32.0, MUL))
    ts(T.c1[:, :], T.ic[:, 0:32], T.fa[:, 4:5], SUB)
    ts(T.fa[:, 5:6], T.fa[:, 1:2], 33.0, MUL)
    ts(T.fa[:, 6:7], T.fa[:, 1:2], 64.0, MUL, -64.0, ADD)
    ts(T.fa[:, 7:8], T.fa[:, 1:2], -1.0, ADD, T.fa[:, 4:5], MUL)
    ts(T.hm[:, :], T.k4[:, :], T.fa[:, 2:3], NE, 4096.0, MUL)
    for t in (T.r16, T.r128, T.one):
        v = vec(V.memset(t[:, :], 1.0))
    vec(V.memset(T.tt[:, :], 0.0))
    for k in range(4):
        ts(T.od[:, k:k + 1], T.fa[:, 1:2], 16.0 * (k // 2), ADD)
    for b in range(4):
        vec(V.memset(T.kc[:, b:b + 1], float(start_of(bitrev(b)) + 96 + 2048 * (start_of(bitrev(b + 4)) + 96))))
    vw(v)
    vec(V.memset(T.r16[:, 0:32:16], 0.0))
    vec(V.memset(T.r128[:, 0:128:32], 0.0))
    for k in (1, 0, 3):
        pack(k)

    half = lambda t, k: t[:, 32 * k:32 * k + 32]
    blk = lambda c: bitrev(cores.index(c))
    beats = lambda k, c, other: tt(half(T.cc, k), own, other, GT if cores.index(c) < rank else GE)
    m1 = lambda j: tt(half(T.m1, j), R(j), R(j + 4), MAX)
    b0 = lambda j: tt(half(T.b0, j), R(j + 4), R(j), GT)
    m2 = lambda j: tt(half(T.m2, j), half(T.m1, j), half(T.m1, j + 2), MAX)
    b2 = lambda j: tt(half(T.b2, j), half(T.m1, j + 2), half(T.m1, j), GT)
    j0, jx, jy, jz = me & 3, blk(arrive[1]) & 3, blk(arrive[3]) & 3, blk(arrive[5]) & 3
    order = arrive[:5] + [mate] + arrive[5:]
    won = lambda k: half(T.acc if k else T.cc, k)
    both = lambda k: tt(won(k), won(k - 1), half(T.cc, k), MUL)

    def compare(k):
        V.wait_ge(sem_of(order[k]), n_near if order[k] == mate else n_far)
        return beats(k, order[k], R(blk(order[k])))

    vw(n["v"])
    compare(0)
    pack(2)
    for k in (1, 2):
        v = compare(k)
        (m1, b0)[k - 1](jx)
        vw(v)
        both(k)
    v = compare(3)
    for k in (4, 5):
        compare(k)
        vw(v)
        v = both(k - 1)
    m1(jy)
    vw(v)
    both(5)
    v = compare(6)
    m1(jz)
    vw(v)
    v_e = both(6)
    e = won(6)
    m1(j0)
    b0(j0)
    vw(v_e)
    v_cs = scan(T.cs[:, :], T.one[:, :], e, ADD, SUB)
    tt(T.v1[:, :], e, T.c1[:, :], MUL)
    b0(jz)
    vw(v_cs)
    A.wait_ge(S.v, ts(T.oc[:, 0:1], T.cs[:, 31:32], T.fa[:, 5:6], ADD))
    A.wait_ge(S.s, s_tb)
    s_pre = inc("s", A.activation(T.t1[:, :], T.tb[:, 0:528].indirect(T.oc[:, 0:1]), RELU, bias=T.fa[:, 6:7], accum_out=T.t2[:, 0:1]))
    v = m2(jz & 1)
    vw(v_cs + 1)
    tt(T.v3[:, :], T.v1[:, :], T.cs[:, :], ADD)
    m2(1 - (jz & 1))
    b2(jz & 1)
    A.wait_ge(S.v, b0(jy))
    inc("s", A.activation(T.b1[:, :], T.b0[:, :], SAME, bias=1.0, scale=2047.0))
    inc("s", A.activation(T.bi[:, :], T.b0[:, :], SAME, bias=1.0, scale=1.0 / 2048 - 1.0))
    vw(v + 2)
    V.wait_ge(S.s, s_pre)
    v_ow = ts(T.ow[:, :], T.v3[:, :], T.t2[:, 0:1], ADD, T.fa[:, 7:8], SUB)
    tt(half(T.e3b, 0), half(T.m2, 0), half(T.m2, 1), GE)
    tt(half(T.e3b, 1), half(T.m2, 1), half(T.m2, 0), GT)
    vw(v_ow)
    v_l = vec(V.tensor_copy(T.l[:, 0:528].indirect(T.ow[:, 0:32]), T.cj[:, :]))
    z = jz & 1
    upper = lambda k: tt(half(T.g2, 2 + k), half(T.e3b, k), half(T.b2, k), MUL)
    lower = lambda k: tt(half(T.g2, k), half(T.e3b, k), half(T.g2, 2 + k), SUB)
    vw(v_l - 1)
    b2(1 - z)
    upper(z)
    vw(v_l)
    v_ls = scan(T.ls[:, :], T.hm[:, :], T.l[:, 417:513], MIN, MAX)
    vw(v_ls - 1)
    upper(1 - z)
    vw(v_ls)
    v_og = ts(T.og[:, :], T.ls[:, 3:96:4], T.fa[:, 0:1], ADD)
    A.wait_ge(S.v, v_og)
    s_h = inc("s", A.activation(T.h[:, h0 + 192:h0 + 384], T.xs[:, 0:2048].indirect(T.og[:, 12:24]), COPY))
    lower(z)
    vw(v_og)
    v_h = vec(V.tensor_copy(T.h[:, h0:h0 + 192], T.xs[:, 0:2048].indirect(T.og[:, 0:12])))
    lower(1 - z)
    vw(v_h)
    V.wait_ge(S.s, s_h)
    c0, cq = 32 + 96 * pos, 128 * pos
    v_q = vec(V.quantize_mx(T.ca[:, cq:cq + 128], T.pa[:, 480 + cq:480 + cq + 128], T.h[:, :]))
    g.wait_ge(S.v, v_q)
    by = lambda t, a, w=96: t[:, a:a + w].bitcast(dt.uint8)
    wide = T.pa[:, 224 + 384 * pos:608 + 384 * pos]
    codes_of = lambda c: S["b%d" % cores.index(c)]
    send((eng_far, codes_of(core), by(T.ca, c0), [(c, by(T.cb, col(core, c))) for c in same]), (eng_near, S.aap, wide, [(mate, wide)]))
    send((eng_near, S.aa, by(T.ca, c0), [(mate, by(T.ca, c0))]))
    g.wait_ge(S.aap, n_near)
    planes_of = lambda c: S["c%d" % cores.index(c)]
    send((eng_far, planes_of(core), T.pa[:, 512:704], [(c, T.pb[:, slot(core, c):slot(core, c) + 192]) for c in same]))
    direct = arrive[::2]
    for k, c in enumerate(direct):
        g.wait_ge(codes_of(c), n_far)
        send((eng_near, S["ac%d" % k], by(T.cb, col(c)), [(mate, by(T.cb, col(c)))]))

    freed = [None] * 8
    bank = [0]

    def product(q, codes, plane, a, w, skip, keep, at, by_vector=False):
        b = bank[0]
        bank[0] = (b + 1) % 8
        if freed[b]:
            P.wait_ge(*freed[b])
        c = 512 * b
        k = inc("pe", P.matmul_mx(T.ps[:, c:c + w], T.cw[:, 128 * q:128 * q + 128], T.pw[:, 128 * q:128 * q + 128],
                                  codes[:, a:a + w], plane[0][:, plane[1] + a:plane[1] + a + w], True, True))
        out, res = T.p[:, 768 * q + at:768 * q + at + keep], T.ps[:, c + skip:c + skip + keep]
        (V if by_vector else A).wait_ge(S.pe, k)
        freed[b] = (S.v, vec(V.tensor_copy(out, res))) if by_vector else (S.s, inc("s", A.activation(out, res, COPY)))
        return freed[b]

    def near(a, skip, at):
        for q in range(8):
            product(q, T.ca, (T.pa, 480), a, 128, skip, 96, at)

    P.wait_ge(S.v, v_q)
    near(cq, c0 - cq, 96 * pos)
    P.wait_ge(S.aap, n_near)
    P.wait_ge(S.aa, n_near)
    near(96 - 64 * pos, 32 - 32 * pos, 96 - 96 * pos)

    def chain(links, beside):
        v = v_q - 1
        for k, link in enumerate(links):
            vw(v)
            v = link()
            if k < len(beside) and beside[k]:
                beside[k]()
        return v

    v = chain([
        lambda: tt(T.ee[:, :], T.g2[:, :], T.b1[:, :], MUL),
        lambda: scan(T.cs4[:, :], T.r128[:, :], T.ee[:, :], MUL, SUB),
        lambda: vec(V.tensor_copy(T.tt[:, 0:4], T.cs4[:, 31:128:32])),
        lambda: vec(V.transpose(T.tu[:, :], T.tt[:, :])),
        lambda: scan(T.tv[:, :], T.r16[:, :], T.tu[:, :]),
        lambda: vec(V.transpose(T.tw[:, :], T.tv[:, :])),
        lambda: tt(T.ee[:, 0:128:32], T.st2[:, :], T.tw[:, 0:4], SUB),
        lambda: scan(T.u[:, :], T.r128[:, :], T.ee[:, :], MUL, SUB),
        lambda: tt(T.uv[:, :], T.u[:, :], T.gs[:, :], MUL),
        lambda: tt(T.x1[:, :], T.uv[:, 0:64], T.uv[:, 64:128], ADD),
        lambda: tt(T.xi[:, :], T.x1[:, 0:32], T.x1[:, 32:64], ADD),
        lambda: ts(T.xj[:, :], T.xi[:, :], 2047, AND),
    ], [
        None,
        lambda: tt(T.st1[:, :], T.ee[:, 0:128:32], T.kc[:, :], SUB),
        lambda: tt(T.gs[:, 0:64], T.g2[:, 0:64], T.bi[:, 0:64], MUL),
        lambda: tt(T.st2[:, :], T.st1[:, :], T.tt[:, 0:4], ADD),
        lambda: tt(T.gs[:, 64:128], T.g2[:, 64:128], T.bi[:, 64:128], MUL),
    ])
    vw(v)
    vw(vec(V.tensor_copy(T.dd[:, :], T.xj[:, 0:32].indirect(T.od[:, 0:4]))))
    vw(vec(V.transpose(T.td[:, :], T.dd[:, :])))
    vec(V.tensor_copy(T.off[:, 0:64:2], T.td[:, 0:32]))
    v_off = vec(V.tensor_copy(T.off[:, 1:64:2], T.td[:, 32:64]))

    def turn(k, sem):
        Y.dma_start(T.off[0:128 - 32 * k, 64 * k:64 * k + 64], T.off[32 * k:128, 0:64]).then_inc(sem, 16)
        Y.dma_start(T.off[128 - 32 * k:128, 64 * k:64 * k + 64], T.off[0:32 * k, 0:64]).then_inc(sem, 16)

    Y.wait_ge(S.v, v_off)
    turn(1, S.l1)

    Y.wait_ge(planes_of(direct[2]), n_far)
    turn(2, S.l2)
    turn(3, S.l2)
    pick_of = lambda q, a, b: T.p[:, 768 * q:768 * q + 768].indirect(T.off[:, 32 * q + a // 16:32 * q + b // 16])
    ready = [[], [], []]
    chip = lambda q, c, by_vector: ready[q].append(product(q, T.cb, (T.pb, 0), slot(c, core), 192, 0, 192, 160 + slot(c, core), by_vector))
    for k, c in enumerate(direct):
        P.wait_ge(codes_of(c), n_far)
        P.wait_ge(S["ac%d" % k], n_near)
        P.wait_ge(planes_of(c), n_far)
        if k < 2:
            for q in range(3 - k):
                chip(q, c, q == 2 - k)
        else:
            for j in range(2):
                a = slot(c, core) + 64 * j
                ready[0].append(product(0, T.cb, (T.pb, 0), a, 128, 32 * j, 96, 160 + a + 32 * j, j == 1))
            chip(1, c, False)
    for q in range(8):
        if q == 2:
            chip(q, direct[1], False)
            chip(q, direct[2], False)
        elif q > 2:
            ready.append([product(q, T.cb, (T.pb, 0), 32 + 288 * k, 288, 0, 288, 192 + 288 * k) for k in range(2)])
        if q == 1:
            A.wait_ge(S.v, v_off)
            for sem, k in ready[0]:
                A.wait_ge(sem, k)
            s_half = inc("s", A.activation(T.ya[:, 256:512], pick_of(0, 256, 512), COPY))

    A.wait_ge(S.s, inc("s", A.activation(T.win[:, :], T.rk[:, 0:768].indirect(T.off[:, 0:64]), COPY)))
    A.dma_start(T.wn[:, :], T.win[0:128:32, :]).then_inc(S.st, 16)

    def pick(q, a, b, last):
        out = T.ya[:, a:b]
        for sem, k in ready[q]:
            V.wait_ge(sem, k)
        if last:
            vw(last)
        return vec(V.tensor_tensor(out, pick_of(q, a, b), out, ADD) if last else V.tensor_copy(out, pick_of(q, a, b)))

    vw(v_off)
    last = [pick(0, 0, 256, 0), n["v"]]
    for q in range(1, 8):
        if q in (2, 4):
            V.wait_ge(*((S.l1, 32) if q == 2 else (S.l2, 64)))
        for k in range(2):
            if (q, k) == (1, 1):
                V.wait_ge(S.s, s_half)
            last[k] = pick(q, 256 * k, 256 * k + 256, last[k])
    for k in range(2):
        Y.wait_ge(S.v, last[k])
        Y.dma_start(T.y[:, 256 * k:256 * k + 256], T.ya[:, 256 * k:256 * k + 256]).then_inc(S.st, 16)
    Y.wait_ge(S.st, 48)
    g.wait_ge(S.loc, n["loc"])
    g.wait_ge(S.v, n["v"])
    g.wait_ge(S.s, n["s"])
    g.wait_ge(S.pe, n["pe"])
